import numpy as np
import ml_dtypes


def mxq(x, axis, fmt="e4m3"):
    dtype, down = {"e4m3": (ml_dtypes.float8_e4m3fn, 7), "e5m2": (ml_dtypes.float8_e5m2, 14)}[fmt]
    v = np.moveaxis(np.asarray(x, np.float32).astype(ml_dtypes.bfloat16).astype(np.float64), axis, -1)
    blocks = v.reshape(v.shape[:-1] + (-1, 32))
    amax = np.abs(blocks).max(-1, keepdims=True)
    byte = np.maximum(np.where(amax > 0, np.frexp(amax)[1] - 1 + 127, 0) - down, 1)
    scale = np.exp2(byte - 127.0)
    codes = (blocks / scale).astype(np.float32).astype(dtype).astype(np.float64)
    return np.moveaxis((codes * scale).reshape(v.shape), -1, axis)


WIDE = False


def mx_kscale(k):
    if not WIDE:
        return np.ones(k)
    levels = np.array([18, -18])
    if k % 512:
        return np.exp2(np.random.permutation(np.resize(levels, k // 32))).repeat(32)
    a = np.empty((k // 512, 16))
    for p in range(k // 512):
        a[p, :8] = np.random.permutation(np.resize(levels, 8))
        for g in range(8):
            far = levels[np.abs(levels - a[p, g]) >= 10]
            a[p, g + 8] = far[np.random.randint(len(far))]
    return np.exp2(a.ravel()).repeat(32)


def f64(x):
    return np.asarray(x).astype(np.float64)


def striped(idx):
    return np.tile(np.asarray(idx).reshape(-1, 16).T, (8, 1)).astype(np.uint16)


def unstriped(offs):
    return offs[:16].T.reshape(-1).astype(np.int64)

def planes(y):
    n, m = y.shape
    v = y.astype(np.float32).astype(ml_dtypes.bfloat16).astype(np.float64).reshape(n // 32, 32, m)
    top = np.abs(v).max(1)
    byte = np.clip(np.where(top > 0, np.frexp(top)[1] - 1 + 127 - 7, 1), 1, 254)
    codes = (v * np.exp2(127.0 - byte)[:, None, :]).reshape(n, m).astype(np.float32).astype(ml_dtypes.float8_e4m3fn).view(np.uint8)
    words = codes.reshape(n // 512, 128, 4, m).transpose(0, 1, 3, 2)
    return np.ascontiguousarray(words), np.ascontiguousarray(byte.astype(np.uint8).reshape(n // 512, 16, m))


def setup_inputs():
    n = np.random.standard_normal
    uni = np.random.uniform
    idx = np.random.permutation(2048)[:512]
    f_d = mx_kscale(512)
    f_r = mx_kscale(512)
    return {
        "xT": (0.35 * n((512, 512)) * f_d[:, None] * f_r[None, :]).astype(np.float32),
        "dT": (n((512, 2048)) / np.sqrt(512) / f_d[:, None]).astype(np.float32),
        "us": (uni(0.75, 1.3, (512, 1)) / f_r[:, None]).astype(np.float32),
        "ts": np.tile(uni(0.75, 1.3, 2048), (128, 1)).astype(np.float32),
        "lk": (uni(0.5, 1.5, (512, 512))).astype(np.float32),
        "wt": (uni(0.75, 1.3, (512, 1))).astype(np.float32),
        "offs": striped(idx),
    }


def reference(xT, dT, us, ts, lk, wt, offs):
    idx = unstriped(offs)
    dT_i = f64(dT)[:, idx]
    ts_i = f64(ts)[:1][:, idx]
    a = mxq(f64(xT), 0, "e4m3").T @ mxq(dT_i, 0, "e4m3")
    z = f64(us) * ts_i * a
    m = (z).max(-1, keepdims=True)
    e = np.exp(z - m)
    t1 = (e).sum(-1, keepdims=True)
    f = e * f64(lk)
    t2 = (f).sum(-1, keepdims=True)
    g = f64(wt) * f64(us) * ts_i * (e / t1 - f / t2)
    dd = mxq(f64(xT), 1, "e4m3") @ mxq(g, 0, "e5m2")
    out_0 = np.zeros((512, 2048))
    out_0[:, idx] = dd
    return (out_0,) + planes(out_0)

@@ -1,0 +1,239 @@
+from contextlib import ExitStack
+
+import concourse.mybir as mybir
+from concourse.masks import make_identity
+
+D, R, SLOTS, DOCS = 512, 512, 512, 2048
+FLOPS = 2 * 2 * D * R * SLOTS
+
+F32 = mybir.dt.float32
+BF16 = mybir.dt.bfloat16
+I32 = mybir.dt.int32
+U32 = mybir.dt.uint32
+U16 = mybir.dt.uint16
+U8 = mybir.dt.uint8
+E4M3X4 = mybir.dt.float8_e4m3fn_x4
+E5M2X4 = mybir.dt.float8_e5m2_x4
+ALU = mybir.AluOpType
+ACT = mybir.ActivationFunctionType
+AX = mybir.AxisListType
+
+P = 128
+LANES = 4
+BANK = 512
+RUN = 4
+GRAIN = 256
+GRAINS = DOCS // GRAIN
+GROUPS = [(0, 1), (1, 2), (2, 4), (4, 6), (6, 7), (7, 8)]
+SCALAR_WEAVES = 2
+
+
+def tile_attend_grag_d_pl_kernel(tc, xT, dT, us, ts, lk, wt, offs, out_0, out_1, out_2):
+    nc = tc.nc
+    with ExitStack() as ctx:
+        sb = ctx.enter_context(tc.tile_pool(name="sb", bufs=1))
+        psum = ctx.enter_context(tc.psum_pool(name="psum", bufs=1))
+
+        def bank(b, name):
+            return psum.tile([P, BANK], F32, name=name, tag="bank%d" % b)
+
+        offsets = sb.tile([P, SLOTS // 16], U16, name="offsets")
+        x_raw = sb.tile([P, LANES, R], F32, name="x_raw")
+        ts_cols = sb.tile([P, DOCS // P], F32, name="ts_cols")
+        us_sb = sb.tile([P, LANES], F32, name="us_sb")
+        wt_sb = sb.tile([P, LANES], F32, name="wt_sb")
+        lk_sb = sb.tile([P, LANES, SLOTS], F32, name="lk_sb")
+        docs = [sb.tile([P, DOCS], F32, name="docs%d" % t) for t in range(LANES)]
+
+        nc.scalar.dma_start(out=ts_cols[:], in_=ts[0:1, :].rearrange("o (p m) -> (o p) m", p=P))
+        nc.sync.dma_start(out=x_raw[:], in_=xT.rearrange("(p t) r -> p t r", t=LANES))
+        nc.sync.dma_start(offsets[:], offs)
+        d_rows = dT.rearrange("(p t) c -> p t c", t=LANES)
+        for t in range(LANES):
+            nc.sync.dma_start(out=docs[t][:], in_=d_rows[:, t, :])
+        nc.sync.dma_start(out=lk_sb[:], in_=lk.rearrange("(p j) i -> p j i", j=LANES))
+        nc.scalar.dma_start(out=us_sb[:], in_=us.rearrange("(p j) o -> p (j o)", j=LANES))
+        nc.scalar.dma_start(out=wt_sb[:], in_=wt.rearrange("(p j) o -> p (j o)", j=LANES))
+
+        ident = sb.tile([P, P], F32, name="ident")
+        make_identity(nc, ident[:])
+
+        windows = [sb.tile([P, DOCS], F32, name="window%d" % j) for j in range(LANES)]
+        for j in range(LANES):
+            (nc.vector if j < 2 else nc.gpsimd).memset(windows[j][:], 0.0)
+
+        ts_all = sb.tile([P, DOCS], F32, name="ts_all")
+        per = DOCS // P
+        ts_view = ts_all[:].rearrange("q (p m) -> q p m", m=per)
+        for b in range(per // RUN):
+            spread = bank(b, "spread%d" % b)
+            for m in range(RUN):
+                col = RUN * b + m
+                nc.tensor.transpose(spread[:, P * m : P * (m + 1)], ts_cols[:, col : col + 1].to_broadcast([P, P]), ident[:])
+            nc.scalar.copy(out=ts_view[:, :, RUN * b : RUN * (b + 1)], in_=spread[:].rearrange("q (m p) -> q p m", m=RUN))
+        ts_g = sb.tile([P, SLOTS], F32, name="ts_g")
+        nc.vector.tensor_copy(ts_g[:], ts_all[:].indirect(offsets[:]))
+
+        xd = sb.tile([P, LANES, P, LANES], BF16, name="xd", align_bytes=64)
+        nc.scalar.copy(out=xd[:].rearrange("p j s t -> p s t j"), in_=x_raw[:].rearrange("p t (s j) -> p s t j", j=LANES))
+        xd_codes = sb.tile([P, R], U32, name="xd_codes", align_bytes=64)
+        xd_scales = sb.tile([P, R], U8, name="xd_scales", align_bytes=64)
+        nc.vector.quantize_mx(out=xd_codes[:].bitcast(E4M3X4), scales=xd_scales[:], in_=xd[:].rearrange("p j s t -> p (j s t)"))
+
+        xr = sb.tile([P, LANES, P, LANES], BF16, name="xr", align_bytes=64)
+        for j in range(LANES):
+            turned = bank(LANES + j, "turned%d" % j)
+            for t in range(LANES):
+                nc.tensor.transpose(turned[:, P * t : P * (t + 1)], x_raw[:, j, t::LANES], ident[:])
+            nc.scalar.copy(out=xr[:, j, :, :], in_=turned[:].rearrange("s (t p) -> s p t", t=LANES))
+        xr_codes = sb.tile([P, D], U32, name="xr_codes", align_bytes=64)
+        xr_scales = sb.tile([P, D], U8, name="xr_scales", align_bytes=64)
+        nc.vector.quantize_mx(out=xr_codes[:].bitcast(E4M3X4), scales=xr_scales[:], in_=xr[:].rearrange("p j s t -> p (j s t)"))
+
+        wu = sb.tile([P, LANES], F32, name="wu")
+        nc.vector.tensor_tensor(wu[:], wt_sb[:], us_sb[:], ALU.mult)
+
+        half = SLOTS // 2
+        halves = [slice(half * h, half * (h + 1)) for h in range(2)]
+        dg = sb.tile([P, SLOTS * LANES], BF16, name="dg", align_bytes=64)
+        dg_lanes = dg[:].rearrange("p (i t) -> p i t", t=LANES)
+        for t in range(LANES - 1):
+            nc.vector.tensor_copy(dg_lanes[:, :, t], docs[t][:].indirect(offsets[:]))
+        for h in range(2):
+            nc.vector.tensor_copy(dg_lanes[:, halves[h], LANES - 1], docs[LANES - 1][:].indirect(offsets[:, 16 * h : 16 * (h + 1)]))
+        dg_codes = sb.tile([P, SLOTS], U32, name="dg_codes", align_bytes=64)
+        dg_scales = sb.tile([P, SLOTS], U8, name="dg_scales", align_bytes=64)
+        for h in range(2):
+            nc.vector.quantize_mx(out=dg_codes[:, halves[h]].bitcast(E4M3X4), scales=dg_scales[:, halves[h]],
+                                  in_=dg[:, LANES * half * h : LANES * half * (h + 1)])
+
+        def score(acc, j, slots):
+            cols = slice(P * j, P * (j + 1))
+            nc.tensor.matmul_mx(out=acc, lhsT=xd_codes[:, cols].bitcast(E4M3X4), lhsT_scale=xd_scales[:, cols],
+                                rhs=dg_codes[:, slots].bitcast(E4M3X4), rhs_scale=dg_scales[:, slots], start=True, stop=True)
+
+        scores = [bank(b, "scores%d" % b) for b in range(LANES)]
+        for h in range(2):
+            for j in range(2):
+                score(scores[h][:, halves[j]], j, halves[h])
+        for j in range(2, LANES):
+            score(scores[j][:], j, slice(0, SLOTS))
+
+        z = [sb.tile([P, SLOTS], F32, name="z%d" % j) for j in range(LANES)]
+        e = [sb.tile([P, SLOTS], F32, name="e%d" % j) for j in range(LANES)]
+        f = [sb.tile([P, SLOTS], F32, name="f%d" % j) for j in range(LANES)]
+        neg_max = [sb.tile([P, 1], F32, name="neg_max%d" % j) for j in range(LANES)]
+        sums = [sb.tile([P, 4], F32, name="sums%d" % h) for h in range(2)]
+        inv = [sb.tile([P, 4], F32, name="inv%d" % h) for h in range(2)]
+        et = sb.tile([P, LANES, SLOTS], F32, name="et")
+        hh = sb.tile([P, LANES, SLOTS], F32, name="hh")
+
+        def scale_scores(j, acc, slots):
+            nc.vector.scalar_tensor_tensor(z[j][:, slots], acc, us_sb[:, j : j + 1], ts_g[:, slots], ALU.mult, ALU.mult)
+
+        def row_max(j):
+            nc.vector.tensor_reduce(neg_max[j][:], z[j][:], AX.X, ALU.max, negate=True)
+            c = 2 * (j % 2)
+            nc.scalar.activation(e[j][:], z[j][:], ACT.Exp, bias=neg_max[j][:], scale=1.0, accum_out=sums[j // 2][:, c : c + 1])
+
+        def lik_sum(j):
+            c = 2 * (j % 2) + 1
+            nc.vector.scalar_tensor_tensor(f[j][:], e[j][:], -1.0, lk_sb[:, j, :], ALU.mult, ALU.mult, accum_out=sums[j // 2][:, c : c + 1])
+
+        def factors(h):
+            nc.vector.reciprocal(inv[h][:], sums[h][:])
+            for j in (2 * h, 2 * h + 1):
+                c = 2 * (j % 2)
+                nc.scalar.activation(hh[:, j, :], lk_sb[:, j, :], ACT.Identity, bias=inv[h][:, c : c + 1], scale=inv[h][:, c + 1 : c + 2])
+
+        def scaled_e(j):
+            nc.vector.scalar_tensor_tensor(et[:, j, :], e[j][:], wu[:, j : j + 1], ts_g[:], ALU.mult, ALU.mult)
+
+        for h in range(2):
+            for j in range(2):
+                scale_scores(j, scores[h][:, halves[j]], halves[h])
+        row_max(0)
+        row_max(1)
+        for j in range(2, LANES):
+            scale_scores(j, scores[j][:], slice(0, SLOTS))
+        row_max(2)
+        row_max(3)
+        lik_sum(0)
+        lik_sum(1)
+        lik_sum(2)
+        factors(0)
+        lik_sum(3)
+        scaled_e(0)
+        factors(1)
+        scaled_e(1)
+        scaled_e(2)
+        scaled_e(3)
+
+        g = sb.tile([P, SLOTS, LANES], BF16, name="g", align_bytes=64)
+        g_codes = sb.tile([P, SLOTS], U32, name="g_codes", align_bytes=64)
+        g_scales = sb.tile([P, SLOTS], U8, name="g_scales", align_bytes=64)
+        for h in range(2):
+            cols = halves[h]
+            nc.vector.tensor_tensor(g[:, cols, :].rearrange("p (c i) j -> p c j i", i=RUN),
+                                    et[:, :, cols].rearrange("p j (c i) -> p c j i", i=RUN),
+                                    hh[:, :, cols].rearrange("p j (c i) -> p c j i", i=RUN), ALU.mult)
+        for h in range(2):
+            cols = slice(half * h, half * (h + 1))
+            nc.vector.quantize_mx(out=g_codes[:, cols].bitcast(E5M2X4), scales=g_scales[:, cols], in_=g[:, cols, :].rearrange("p i j -> p (i j)"))
+
+        out_rows = out_0.rearrange("(p j) c -> p j c", j=LANES)
+        pairs = sb.tile([P, DOCS * LANES], BF16, name="pairs")
+        pair_lanes = pairs[:].rearrange("p (k u c e) -> p k u c e", u=2, c=GRAIN, e=2)
+
+        def round_lane(j, k0, k1):
+            nc.scalar.copy(out=pair_lanes[:, k0:k1, j // 2, :, j % 2],
+                           in_=windows[j][:, GRAIN * k0 : GRAIN * k1].rearrange("p (k c) -> p k c", c=GRAIN))
+
+        dd = [sb.tile([P, SLOTS], F32, name="dd%d" % j) for j in range(LANES)]
+        for j in range(LANES):
+            acc = bank(LANES + j, "grad%d" % j)
+            cols = slice(P * j, P * (j + 1))
+            nc.tensor.matmul_mx(out=acc[:], lhsT=xr_codes[:, cols].bitcast(E4M3X4), lhsT_scale=xr_scales[:, cols],
+                                rhs=g_codes[:].bitcast(E5M2X4), rhs_scale=g_scales[:], start=True, stop=True)
+            nc.scalar.copy(out=dd[j][:], in_=acc[:])
+        for j in range(LANES):
+            nc.vector.tensor_copy(windows[j][:].indirect(offsets[:]), dd[j][:])
+            nc.sync.dma_start(out=out_rows[:, j, :], in_=windows[j][:])
+            for k0, k1 in (GROUPS if j == LANES - 1 else [(0, GRAINS)]):
+                round_lane(j, k0, k1)
+
+        words_out = out_1.rearrange("a p c l -> p (a c l)").bitcast(I32)
+        scales_out = out_2.rearrange("a f c -> (a f) c").bitcast(I32)
+        y_scales = sb.tile([P, DOCS], U8, name="y_scales", align_bytes=64)
+        woven = sb.tile([P, DOCS * LANES], BF16, name="woven", align_bytes=64)
+        y_codes = sb.tile([P, DOCS], U32, name="y_codes", align_bytes=64)
+
+        def weave(n):
+            k0, k1 = GROUPS[n]
+            span = slice(GRAIN * LANES * k0, GRAIN * LANES * k1)
+            on_scalar = n >= len(GROUPS) - SCALAR_WEAVES
+            word = U32 if on_scalar else I32
+            dst = woven[:, span].bitcast(word).rearrange("p (k c i u) -> p k c u i", c=GRAIN // RUN, i=RUN, u=2)
+            src = pairs[:, span].bitcast(word).rearrange("p (k u c i) -> p k c u i", c=GRAIN // RUN, i=RUN, u=2)
+            if on_scalar:
+                nc.scalar.copy(out=dst, in_=src)
+            else:
+                nc.vector.tensor_copy(out=dst, in_=src)
+
+        def quantise(n):
+            k0, k1 = GROUPS[n]
+            cols = slice(GRAIN * k0, GRAIN * k1)
+            nc.vector.quantize_mx(out=y_codes[:, cols].bitcast(E4M3X4), scales=y_scales[:, cols],
+                                  in_=woven[:, GRAIN * LANES * k0 : GRAIN * LANES * k1])
+            if n > 0:
+                first = 0 if n == 1 else GRAIN * k0
+                nc.sync.dma_start(out=words_out[:, first : GRAIN * k1], in_=y_codes[:, first : GRAIN * k1].bitcast(I32))
+
+        weave(0)
+        for n in range(1, len(GROUPS)):
+            weave(n)
+            quantise(n - 1)
+        quantise(len(GROUPS) - 1)
+        for q in range(4):
+            eng = nc.scalar if q % 2 else nc.sync
+            eng.dma_start(out=scales_out[4 * q : 4 * q + 4, :], in_=y_scales[32 * q : 32 * q + 4, :].bitcast(I32))

@@ -48,12 +48,12 @@ def tile_attend_grag_d_pl_kernel(tc, xT, dT, us, ts, lk, wt, offs, out_0, out_1,
         nc.scalar.dma_start(out=ts_cols[:], in_=ts[0:1, :].rearrange("o (p m) -> (o p) m", p=P))
         nc.sync.dma_start(out=x_raw[:], in_=xT.rearrange("(p t) r -> p t r", t=LANES))
         nc.sync.dma_start(offsets[:], offs)
+        nc.sync.dma_start(out=us_sb[:], in_=us.rearrange("(p j) o -> p (j o)", j=LANES))
+        nc.sync.dma_start(out=wt_sb[:], in_=wt.rearrange("(p j) o -> p (j o)", j=LANES))
         d_rows = dT.rearrange("(p t) c -> p t c", t=LANES)
         for t in range(LANES):
             nc.sync.dma_start(out=docs[t][:], in_=d_rows[:, t, :])
         nc.sync.dma_start(out=lk_sb[:], in_=lk.rearrange("(p j) i -> p j i", j=LANES))
-        nc.scalar.dma_start(out=us_sb[:], in_=us.rearrange("(p j) o -> p (j o)", j=LANES))
-        nc.scalar.dma_start(out=wt_sb[:], in_=wt.rearrange("(p j) o -> p (j o)", j=LANES))
 
         ident = sb.tile([P, P], F32, name="ident")
         make_identity(nc, ident[:])
@@ -75,10 +75,11 @@ def tile_attend_grag_d_pl_kernel(tc, xT, dT, us, ts, lk, wt, offs, out_0, out_1,
         nc.vector.tensor_copy(ts_g[:], ts_all[:].indirect(offsets[:]))
 
         xd = sb.tile([P, LANES, P, LANES], BF16, name="xd", align_bytes=64)
-        nc.scalar.copy(out=xd[:].rearrange("p j s t -> p s t j"), in_=x_raw[:].rearrange("p t (s j) -> p s t j", j=LANES))
+        for u in range(2):
+            nc.scalar.copy(out=xd[:, 2 * u : 2 * u + 2].rearrange("p j s t -> p s t j"),
+                           in_=x_raw[:].rearrange("p t (s j) -> p s t j", j=LANES)[:, :, :, 2 * u : 2 * u + 2])
         xd_codes = sb.tile([P, R], U32, name="xd_codes", align_bytes=64)
         xd_scales = sb.tile([P, R], U8, name="xd_scales", align_bytes=64)
-        nc.vector.quantize_mx(out=xd_codes[:].bitcast(E4M3X4), scales=xd_scales[:], in_=xd[:].rearrange("p j s t -> p (j s t)"))
 
         xr = sb.tile([P, LANES, P, LANES], BF16, name="xr", align_bytes=64)
         for j in range(LANES):
@@ -88,7 +89,6 @@ def tile_attend_grag_d_pl_kernel(tc, xT, dT, us, ts, lk, wt, offs, out_0, out_1,
             nc.scalar.copy(out=xr[:, j, :, :], in_=turned[:].rearrange("s (t p) -> s p t", t=LANES))
         xr_codes = sb.tile([P, D], U32, name="xr_codes", align_bytes=64)
         xr_scales = sb.tile([P, D], U8, name="xr_scales", align_bytes=64)
-        nc.vector.quantize_mx(out=xr_codes[:].bitcast(E4M3X4), scales=xr_scales[:], in_=xr[:].rearrange("p j s t -> p (j s t)"))
 
         wu = sb.tile([P, LANES], F32, name="wu")
         nc.vector.tensor_tensor(wu[:], wt_sb[:], us_sb[:], ALU.mult)
@@ -97,8 +97,11 @@ def tile_attend_grag_d_pl_kernel(tc, xT, dT, us, ts, lk, wt, offs, out_0, out_1,
         halves = [slice(half * h, half * (h + 1)) for h in range(2)]
         dg = sb.tile([P, SLOTS * LANES], BF16, name="dg", align_bytes=64)
         dg_lanes = dg[:].rearrange("p (i t) -> p i t", t=LANES)
-        for t in range(LANES - 1):
+        for t in range(LANES - 2):
             nc.vector.tensor_copy(dg_lanes[:, :, t], docs[t][:].indirect(offsets[:]))
+        nc.vector.quantize_mx(out=xd_codes[:].bitcast(E4M3X4), scales=xd_scales[:], in_=xd[:].rearrange("p j s t -> p (j s t)"))
+        nc.vector.tensor_copy(dg_lanes[:, :, LANES - 2], docs[LANES - 2][:].indirect(offsets[:]))
+        nc.vector.quantize_mx(out=xr_codes[:].bitcast(E4M3X4), scales=xr_scales[:], in_=xr[:].rearrange("p j s t -> p (j s t)"))
         for h in range(2):
             nc.vector.tensor_copy(dg_lanes[:, halves[h], LANES - 1], docs[LANES - 1][:].indirect(offsets[:, 16 * h : 16 * (h + 1)]))
         dg_codes = sb.tile([P, SLOTS], U32, name="dg_codes", align_bytes=64)
@@ -169,17 +172,38 @@ def tile_attend_grag_d_pl_kernel(tc, xT, dT, us, ts, lk, wt, offs, out_0, out_1,
         scaled_e(2)
         scaled_e(3)
 
-        g = sb.tile([P, SLOTS, LANES], BF16, name="g", align_bytes=64)
-        g_codes = sb.tile([P, SLOTS], U32, name="g_codes", align_bytes=64)
-        g_scales = sb.tile([P, SLOTS], U8, name="g_scales", align_bytes=64)
-        for h in range(2):
-            cols = halves[h]
-            nc.vector.tensor_tensor(g[:, cols, :].rearrange("p (c i) j -> p c j i", i=RUN),
-                                    et[:, :, cols].rearrange("p j (c i) -> p c j i", i=RUN),
-                                    hh[:, :, cols].rearrange("p j (c i) -> p c j i", i=RUN), ALU.mult)
-        for h in range(2):
-            cols = slice(half * h, half * (h + 1))
-            nc.vector.quantize_mx(out=g_codes[:, cols].bitcast(E5M2X4), scales=g_scales[:, cols], in_=g[:, cols, :].rearrange("p i j -> p (i j)"))
+        g = sb.tile([P, SLOTS * LANES], BF16, name="g", align_bytes=64)
+        g_codes = sb.tile([P, half + SLOTS], U32, name="g_codes", align_bytes=64)
+        g_scales = sb.tile([P, half + SLOTS], U8, name="g_scales", align_bytes=64)
+        nc.gpsimd.memset(g_codes[:, 0:half], 0)
+        nc.gpsimd.memset(g_scales[:, 0:half], 0)
+
+        def gradient(i0, i1):
+            nc.vector.tensor_tensor(g[:, LANES * i0 : LANES * i1].rearrange("p (c i j) -> p c j i", i=2, j=LANES),
+                                    et[:, :, i0:i1].rearrange("p j (c i) -> p c j i", i=2),
+                                    hh[:, :, i0:i1].rearrange("p j (c i) -> p c j i", i=2), ALU.mult)
+
+        def quantise_gradient(i0, i1):
+            nc.vector.quantize_mx(out=g_codes[:, half + i0 : half + i1].bitcast(E5M2X4), scales=g_scales[:, half + i0 : half + i1],
+                                  in_=g[:, LANES * i0 : LANES * i1])
+
+        def table_gradient(acc, j, first):
+            cols = slice(P * j, P * (j + 1))
+            nc.tensor.matmul_mx(out=acc[:], lhsT=xr_codes[:, cols].bitcast(E4M3X4), lhsT_scale=xr_scales[:, cols],
+                                rhs=g_codes[:, first : first + SLOTS].bitcast(E5M2X4), rhs_scale=g_scales[:, first : first + SLOTS],
+                                start=True, stop=True)
+
+        dd = [sb.tile([P, SLOTS], F32, name="dd%d" % j) for j in range(LANES)]
+        quarter = SLOTS // 4
+        gradient(0, half)
+        gradient(half, half + quarter)
+        quantise_gradient(0, half)
+        early = bank(0, "early")
+        table_gradient(early, 0, 0)
+        nc.scalar.copy(out=dd[0][:, halves[0]], in_=early[:, halves[1]])
+        gradient(half + quarter, SLOTS)
+        quantise_gradient(half, half + quarter)
+        quantise_gradient(half + quarter, SLOTS)
 
         out_rows = out_0.rearrange("(p j) c -> p j c", j=LANES)
         pairs = sb.tile([P, DOCS * LANES], BF16, name="pairs")
@@ -189,22 +213,24 @@ def tile_attend_grag_d_pl_kernel(tc, xT, dT, us, ts, lk, wt, offs, out_0, out_1,
             nc.scalar.copy(out=pair_lanes[:, k0:k1, j // 2, :, j % 2],
                            in_=windows[j][:, GRAIN * k0 : GRAIN * k1].rearrange("p (k c) -> p k c", c=GRAIN))
 
-        dd = [sb.tile([P, SLOTS], F32, name="dd%d" % j) for j in range(LANES)]
         for j in range(LANES):
             acc = bank(LANES + j, "grad%d" % j)
-            cols = slice(P * j, P * (j + 1))
-            nc.tensor.matmul_mx(out=acc[:], lhsT=xr_codes[:, cols].bitcast(E4M3X4), lhsT_scale=xr_scales[:, cols],
-                                rhs=g_codes[:].bitcast(E5M2X4), rhs_scale=g_scales[:], start=True, stop=True)
-            nc.scalar.copy(out=dd[j][:], in_=acc[:])
+            table_gradient(acc, j, half)
+            todo = halves[1] if j == 0 else slice(0, SLOTS)
+            nc.scalar.copy(out=dd[j][:, todo], in_=acc[:, todo])
         for j in range(LANES):
-            nc.vector.tensor_copy(windows[j][:].indirect(offsets[:]), dd[j][:])
+            if j == 0:
+                for h in range(2):
+                    nc.vector.tensor_copy(windows[j][:].indirect(offsets[:, 16 * h : 16 * (h + 1)]), dd[j][:, halves[h]])
+            else:
+                nc.vector.tensor_copy(windows[j][:].indirect(offsets[:]), dd[j][:])
             nc.sync.dma_start(out=out_rows[:, j, :], in_=windows[j][:])
             for k0, k1 in (GROUPS if j == LANES - 1 else [(0, GRAINS)]):
                 round_lane(j, k0, k1)
 
         words_out = out_1.rearrange("a p c l -> p (a c l)").bitcast(I32)
-        scales_out = out_2.rearrange("a f c -> (a f) c").bitcast(I32)
-        y_scales = sb.tile([P, DOCS], U8, name="y_scales", align_bytes=64)
+        scales_out = out_2.rearrange("o f (a c) -> a (o f) c", c=BANK).bitcast(I32)
+        y_scales = sb.tile([P, BANK], U8, name="y_scales", align_bytes=64)
         woven = sb.tile([P, DOCS * LANES], BF16, name="woven", align_bytes=64)
         y_codes = sb.tile([P, DOCS], U32, name="y_codes", align_bytes=64)
 
@@ -213,8 +239,8 @@ def tile_attend_grag_d_pl_kernel(tc, xT, dT, us, ts, lk, wt, offs, out_0, out_1,
             span = slice(GRAIN * LANES * k0, GRAIN * LANES * k1)
             on_scalar = n >= len(GROUPS) - SCALAR_WEAVES
             word = U32 if on_scalar else I32
-            dst = woven[:, span].bitcast(word).rearrange("p (k c i u) -> p k c u i", c=GRAIN // RUN, i=RUN, u=2)
-            src = pairs[:, span].bitcast(word).rearrange("p (k u c i) -> p k c u i", c=GRAIN // RUN, i=RUN, u=2)
+            dst = woven[:, span].bitcast(word).rearrange("p (k c i u) -> p k c u i", c=GRAIN // 2, i=2, u=2)
+            src = pairs[:, span].bitcast(word).rearrange("p (k u c i) -> p k c u i", c=GRAIN // 2, i=2, u=2)
             if on_scalar:
                 nc.scalar.copy(out=dst, in_=src)
             else:
@@ -223,7 +249,7 @@ def tile_attend_grag_d_pl_kernel(tc, xT, dT, us, ts, lk, wt, offs, out_0, out_1,
         def quantise(n):
             k0, k1 = GROUPS[n]
             cols = slice(GRAIN * k0, GRAIN * k1)
-            nc.vector.quantize_mx(out=y_codes[:, cols].bitcast(E4M3X4), scales=y_scales[:, cols],
+            nc.vector.quantize_mx(out=y_codes[:, cols].bitcast(E4M3X4), scales=y_scales[4 * (k0 // 2) : P, GRAIN * (k0 % 2) : GRAIN * (k0 % 2 + k1 - k0)],
                                   in_=woven[:, GRAIN * LANES * k0 : GRAIN * LANES * k1])
             if n > 0:
                 first = 0 if n == 1 else GRAIN * k0
@@ -236,4 +262,4 @@ def tile_attend_grag_d_pl_kernel(tc, xT, dT, us, ts, lk, wt, offs, out_0, out_1,
         quantise(len(GROUPS) - 1)
         for q in range(4):
             eng = nc.scalar if q % 2 else nc.sync
-            eng.dma_start(out=scales_out[4 * q : 4 * q + 4, :], in_=y_scales[32 * q : 32 * q + 4, :].bitcast(I32))
+            eng.dma_start(out=scales_out[:, 4 * q : 4 * q + 4, :], in_=y_scales[32 * q : 32 * q + 16, :].bitcast(I32))

@@ -43,16 +43,16 @@ def tile_attend_grag_d_pl_kernel(tc, xT, dT, us, ts, lk, wt, offs, out_0, out_1,
         us_sb = sb.tile([P, LANES], F32, name="us_sb")
         wt_sb = sb.tile([P, LANES], F32, name="wt_sb")
         lk_sb = sb.tile([P, LANES, SLOTS], F32, name="lk_sb")
-        docs = [sb.tile([P, DOCS], F32, name="docs%d" % t) for t in range(LANES)]
+        docs = [sb.tile([P, DOCS], F32, name="docs%d" % t, tag="docs%d" % t, align_bytes=64) for t in range(LANES)]
 
         nc.scalar.dma_start(out=ts_cols[:], in_=ts[0:1, :].rearrange("o (p m) -> (o p) m", p=P))
         nc.sync.dma_start(out=x_raw[:], in_=xT.rearrange("(p t) r -> p t r", t=LANES))
         nc.sync.dma_start(offsets[:], offs)
-        nc.sync.dma_start(out=us_sb[:], in_=us.rearrange("(p j) o -> p (j o)", j=LANES))
-        nc.sync.dma_start(out=wt_sb[:], in_=wt.rearrange("(p j) o -> p (j o)", j=LANES))
         d_rows = dT.rearrange("(p t) c -> p t c", t=LANES)
         for t in range(LANES):
             nc.sync.dma_start(out=docs[t][:], in_=d_rows[:, t, :])
+        nc.sync.dma_start(out=us_sb[:], in_=us.rearrange("(p j) o -> p (j o)", j=LANES))
+        nc.sync.dma_start(out=wt_sb[:], in_=wt.rearrange("(p j) o -> p (j o)", j=LANES))
         nc.sync.dma_start(out=lk_sb[:], in_=lk.rearrange("(p j) i -> p j i", j=LANES))
 
         ident = sb.tile([P, P], F32, name="ident")
@@ -74,24 +74,24 @@ def tile_attend_grag_d_pl_kernel(tc, xT, dT, us, ts, lk, wt, offs, out_0, out_1,
         ts_g = sb.tile([P, SLOTS], F32, name="ts_g")
         nc.vector.tensor_copy(ts_g[:], ts_all[:].indirect(offsets[:]))
 
-        xd = sb.tile([P, LANES, P, LANES], BF16, name="xd", align_bytes=64)
-        for u in range(2):
-            nc.scalar.copy(out=xd[:, 2 * u : 2 * u + 2].rearrange("p j s t -> p s t j"),
-                           in_=x_raw[:].rearrange("p t (s j) -> p s t j", j=LANES)[:, :, :, 2 * u : 2 * u + 2])
+        xd = sb.tile([P, R * LANES], BF16, name="xd", align_bytes=64)
+        nc.vector.tensor_copy(out=xd[:].rearrange("p (j s t) -> p s t j", j=LANES, t=LANES),
+                              in_=x_raw[:].rearrange("p t (s j) -> p s t j", j=LANES))
         xd_codes = sb.tile([P, R], U32, name="xd_codes", align_bytes=64)
         xd_scales = sb.tile([P, R], U8, name="xd_scales", align_bytes=64)
+        nc.vector.quantize_mx(out=xd_codes[:].bitcast(E4M3X4), scales=xd_scales[:], in_=xd[:])
 
-        xr = sb.tile([P, LANES, P, LANES], BF16, name="xr", align_bytes=64)
-        for j in range(LANES):
-            turned = bank(LANES + j, "turned%d" % j)
-            for t in range(LANES):
-                nc.tensor.transpose(turned[:, P * t : P * (t + 1)], x_raw[:, j, t::LANES], ident[:])
-            nc.scalar.copy(out=xr[:, j, :, :], in_=turned[:].rearrange("s (t p) -> s p t", t=LANES))
-        xr_codes = sb.tile([P, D], U32, name="xr_codes", align_bytes=64)
-        xr_scales = sb.tile([P, D], U8, name="xr_scales", align_bytes=64)
+        xd_words = xd[:].bitcast(F32).rearrange("p (j s u) -> p j s u", j=LANES, u=2)
+        xr = sb.tile([P, D * LANES], BF16, name="xr", align_bytes=64)
+        xr_view = xr[:].rearrange("s (t p j) -> s t p j", t=LANES, j=LANES)
+        for u in range(2):
+            turned = bank(LANES + u, "turned%d" % u)
+            for j in range(LANES):
+                nc.tensor.transpose(turned[:, P * j : P * (j + 1)], xd_words[:, j, :, u], ident[:])
+            nc.scalar.copy(out=xr_view[:, 2 * u : 2 * u + 2], in_=turned[:].bitcast(BF16).rearrange("s (j p e) -> s e p j", j=LANES, e=2))
 
         wu = sb.tile([P, LANES], F32, name="wu")
-        nc.vector.tensor_tensor(wu[:], wt_sb[:], us_sb[:], ALU.mult)
+        nc.gpsimd.tensor_tensor(wu[:], wt_sb[:], us_sb[:], ALU.mult)
 
         half = SLOTS // 2
         halves = [slice(half * h, half * (h + 1)) for h in range(2)]
@@ -99,9 +99,10 @@ def tile_attend_grag_d_pl_kernel(tc, xT, dT, us, ts, lk, wt, offs, out_0, out_1,
         dg_lanes = dg[:].rearrange("p (i t) -> p i t", t=LANES)
         for t in range(LANES - 2):
             nc.vector.tensor_copy(dg_lanes[:, :, t], docs[t][:].indirect(offsets[:]))
-        nc.vector.quantize_mx(out=xd_codes[:].bitcast(E4M3X4), scales=xd_scales[:], in_=xd[:].rearrange("p j s t -> p (j s t)"))
+        xr_codes = sb.tile([P, D], U32, name="xr_codes", tag="docs1", align_bytes=64)
+        xr_scales = sb.tile([P, D], U8, name="xr_scales", align_bytes=64)
+        nc.vector.quantize_mx(out=xr_codes[:].bitcast(E4M3X4), scales=xr_scales[:], in_=xr[:])
         nc.vector.tensor_copy(dg_lanes[:, :, LANES - 2], docs[LANES - 2][:].indirect(offsets[:]))
-        nc.vector.quantize_mx(out=xr_codes[:].bitcast(E4M3X4), scales=xr_scales[:], in_=xr[:].rearrange("p j s t -> p (j s t)"))
         for h in range(2):
             nc.vector.tensor_copy(dg_lanes[:, halves[h], LANES - 1], docs[LANES - 1][:].indirect(offsets[:, 16 * h : 16 * (h + 1)]))
         dg_codes = sb.tile([P, SLOTS], U32, name="dg_codes", align_bytes=64)
@@ -115,24 +116,22 @@ def tile_attend_grag_d_pl_kernel(tc, xT, dT, us, ts, lk, wt, offs, out_0, out_1,
             nc.tensor.matmul_mx(out=acc, lhsT=xd_codes[:, cols].bitcast(E4M3X4), lhsT_scale=xd_scales[:, cols],
                                 rhs=dg_codes[:, slots].bitcast(E4M3X4), rhs_scale=dg_scales[:, slots], start=True, stop=True)
 
-        scores = [bank(b, "scores%d" % b) for b in range(LANES)]
-        for h in range(2):
-            for j in range(2):
-                score(scores[h][:, halves[j]], j, halves[h])
-        for j in range(2, LANES):
-            score(scores[j][:], j, slice(0, SLOTS))
+        pieces = [(j, halves[h]) for h in range(2) for j in range(2)] + [(j, slice(0, SLOTS)) for j in range(2, LANES)]
+        scores = [bank(b, "scores%d" % b) for b in range(len(pieces))]
+        for b, (j, slots) in enumerate(pieces):
+            score(scores[b][:, slots], j, slots)
 
         z = [sb.tile([P, SLOTS], F32, name="z%d" % j) for j in range(LANES)]
         e = [sb.tile([P, SLOTS], F32, name="e%d" % j) for j in range(LANES)]
-        f = [sb.tile([P, SLOTS], F32, name="f%d" % j) for j in range(LANES)]
         neg_max = [sb.tile([P, 1], F32, name="neg_max%d" % j) for j in range(LANES)]
         sums = [sb.tile([P, 4], F32, name="sums%d" % h) for h in range(2)]
         inv = [sb.tile([P, 4], F32, name="inv%d" % h) for h in range(2)]
         et = sb.tile([P, LANES, SLOTS], F32, name="et")
         hh = sb.tile([P, LANES, SLOTS], F32, name="hh")
 
-        def scale_scores(j, acc, slots):
-            nc.vector.scalar_tensor_tensor(z[j][:, slots], acc, us_sb[:, j : j + 1], ts_g[:, slots], ALU.mult, ALU.mult)
+        def scale_scores(b):
+            j, slots = pieces[b]
+            nc.vector.scalar_tensor_tensor(z[j][:, slots], scores[b][:, slots], us_sb[:, j : j + 1], ts_g[:, slots], ALU.mult, ALU.mult)
 
         def row_max(j):
             nc.vector.tensor_reduce(neg_max[j][:], z[j][:], AX.X, ALU.max, negate=True)
@@ -141,7 +140,7 @@ def tile_attend_grag_d_pl_kernel(tc, xT, dT, us, ts, lk, wt, offs, out_0, out_1,
 
         def lik_sum(j):
             c = 2 * (j % 2) + 1
-            nc.vector.scalar_tensor_tensor(f[j][:], e[j][:], -1.0, lk_sb[:, j, :], ALU.mult, ALU.mult, accum_out=sums[j // 2][:, c : c + 1])
+            nc.vector.scalar_tensor_tensor(et[:, j, :], e[j][:], -1.0, lk_sb[:, j, :], ALU.mult, ALU.mult, accum_out=sums[j // 2][:, c : c + 1])
 
         def factors(h):
             nc.vector.reciprocal(inv[h][:], sums[h][:])
@@ -152,13 +151,12 @@ def tile_attend_grag_d_pl_kernel(tc, xT, dT, us, ts, lk, wt, offs, out_0, out_1,
         def scaled_e(j):
             nc.vector.scalar_tensor_tensor(et[:, j, :], e[j][:], wu[:, j : j + 1], ts_g[:], ALU.mult, ALU.mult)
 
-        for h in range(2):
-            for j in range(2):
-                scale_scores(j, scores[h][:, halves[j]], halves[h])
+        for b in range(4):
+            scale_scores(b)
         row_max(0)
         row_max(1)
-        for j in range(2, LANES):
-            scale_scores(j, scores[j][:], slice(0, SLOTS))
+        scale_scores(4)
+        scale_scores(5)
         row_max(2)
         row_max(3)
         lik_sum(0)
@@ -179,9 +177,9 @@ def tile_attend_grag_d_pl_kernel(tc, xT, dT, us, ts, lk, wt, offs, out_0, out_1,
         nc.gpsimd.memset(g_scales[:, 0:half], 0)
 
         def gradient(i0, i1):
-            nc.vector.tensor_tensor(g[:, LANES * i0 : LANES * i1].rearrange("p (c i j) -> p c j i", i=2, j=LANES),
-                                    et[:, :, i0:i1].rearrange("p j (c i) -> p c j i", i=2),
-                                    hh[:, :, i0:i1].rearrange("p j (c i) -> p c j i", i=2), ALU.mult)
+            nc.vector.tensor_tensor(g[:, LANES * i0 : LANES * i1].rearrange("p (c i j) -> p c j i", i=RUN, j=LANES),
+                                    et[:, :, i0:i1].rearrange("p j (c i) -> p c j i", i=RUN),
+                                    hh[:, :, i0:i1].rearrange("p j (c i) -> p c j i", i=RUN), ALU.mult)
 
         def quantise_gradient(i0, i1):
             nc.vector.quantize_mx(out=g_codes[:, half + i0 : half + i1].bitcast(E5M2X4), scales=g_scales[:, half + i0 : half + i1],
@@ -196,11 +194,12 @@ def tile_attend_grag_d_pl_kernel(tc, xT, dT, us, ts, lk, wt, offs, out_0, out_1,
         dd = [sb.tile([P, SLOTS], F32, name="dd%d" % j) for j in range(LANES)]
         quarter = SLOTS // 4
         gradient(0, half)
-        gradient(half, half + quarter)
+        gradient(half, half + 64)
         quantise_gradient(0, half)
         early = bank(0, "early")
         table_gradient(early, 0, 0)
         nc.scalar.copy(out=dd[0][:, halves[0]], in_=early[:, halves[1]])
+        gradient(half + 64, half + quarter)
         gradient(half + quarter, SLOTS)
         quantise_gradient(half, half + quarter)
         quantise_gradient(half + quarter, SLOTS)
@@ -239,8 +238,8 @@ def tile_attend_grag_d_pl_kernel(tc, xT, dT, us, ts, lk, wt, offs, out_0, out_1,
             span = slice(GRAIN * LANES * k0, GRAIN * LANES * k1)
             on_scalar = n >= len(GROUPS) - SCALAR_WEAVES
             word = U32 if on_scalar else I32
-            dst = woven[:, span].bitcast(word).rearrange("p (k c i u) -> p k c u i", c=GRAIN // 2, i=2, u=2)
-            src = pairs[:, span].bitcast(word).rearrange("p (k u c i) -> p k c u i", c=GRAIN // 2, i=2, u=2)
+            dst = woven[:, span].bitcast(word).rearrange("p (k c i u) -> p k c u i", c=GRAIN // RUN, i=RUN, u=2)
+            src = pairs[:, span].bitcast(word).rearrange("p (k u c i) -> p k c u i", c=GRAIN // RUN, i=RUN, u=2)
             if on_scalar:
                 nc.scalar.copy(out=dst, in_=src)
             else:

@@ -58,9 +58,9 @@ def tile_attend_grag_d_pl_kernel(tc, xT, dT, us, ts, lk, wt, offs, out_0, out_1,
         ident = sb.tile([P, P], F32, name="ident")
         make_identity(nc, ident[:])
 
-        windows = [sb.tile([P, DOCS], F32, name="window%d" % j) for j in range(LANES)]
-        for j in range(LANES):
-            (nc.vector if j < 2 else nc.gpsimd).memset(windows[j][:], 0.0)
+        windows = [sb.tile([P, DOCS], F32, name="window%d" % j) for j in range(2)]
+        for j in range(2):
+            nc.vector.memset(windows[j][:].bitcast(I32), 0)
 
         ts_all = sb.tile([P, DOCS], F32, name="ts_all")
         per = DOCS // P
@@ -97,8 +97,10 @@ def tile_attend_grag_d_pl_kernel(tc, xT, dT, us, ts, lk, wt, offs, out_0, out_1,
         halves = [slice(half * h, half * (h + 1)) for h in range(2)]
         dg = sb.tile([P, SLOTS * LANES], BF16, name="dg", align_bytes=64)
         dg_lanes = dg[:].rearrange("p (i t) -> p i t", t=LANES)
-        for t in range(LANES - 2):
-            nc.vector.tensor_copy(dg_lanes[:, :, t], docs[t][:].indirect(offsets[:]))
+        dg_flat = sb.tile([P, 2 * SLOTS], BF16, name="dg_flat")
+        for t in range(2):
+            nc.vector.tensor_copy(dg_flat[:, SLOTS * t : SLOTS * (t + 1)], docs[t][:].indirect(offsets[:]))
+        nc.scalar.copy(out=dg_lanes[:, :, 0:2], in_=dg_flat[:].rearrange("p (t i) -> p i t", t=2))
         xr_codes = sb.tile([P, D], U32, name="xr_codes", tag="docs1", align_bytes=64)
         xr_scales = sb.tile([P, D], U8, name="xr_scales", align_bytes=64)
         nc.vector.quantize_mx(out=xr_codes[:].bitcast(E4M3X4), scales=xr_scales[:], in_=xr[:])
@@ -121,7 +123,7 @@ def tile_attend_grag_d_pl_kernel(tc, xT, dT, us, ts, lk, wt, offs, out_0, out_1,
         for b, (j, slots) in enumerate(pieces):
             score(scores[b][:, slots], j, slots)
 
-        z = [sb.tile([P, SLOTS], F32, name="z%d" % j) for j in range(LANES)]
+        z = [sb.tile([P, SLOTS], F32, name="z%d" % j, tag="z%d" % j) for j in range(LANES)]
         e = [sb.tile([P, SLOTS], F32, name="e%d" % j) for j in range(LANES)]
         neg_max = [sb.tile([P, 1], F32, name="neg_max%d" % j) for j in range(LANES)]
         sums = [sb.tile([P, 4], F32, name="sums%d" % h) for h in range(2)]
@@ -159,6 +161,9 @@ def tile_attend_grag_d_pl_kernel(tc, xT, dT, us, ts, lk, wt, offs, out_0, out_1,
         scale_scores(5)
         row_max(2)
         row_max(3)
+        for j in range(2):
+            windows.append(sb.tile([P, DOCS], F32, name="window%d" % (2 + j), tag="z%d" % j))
+            nc.gpsimd.memset(windows[2 + j][:], 0.0)
         lik_sum(0)
         lik_sum(1)
         lik_sum(2)
@@ -194,12 +199,11 @@ def tile_attend_grag_d_pl_kernel(tc, xT, dT, us, ts, lk, wt, offs, out_0, out_1,
         dd = [sb.tile([P, SLOTS], F32, name="dd%d" % j) for j in range(LANES)]
         quarter = SLOTS // 4
         gradient(0, half)
-        gradient(half, half + 64)
+        gradient(half, half + quarter)
         quantise_gradient(0, half)
         early = bank(0, "early")
         table_gradient(early, 0, 0)
         nc.scalar.copy(out=dd[0][:, halves[0]], in_=early[:, halves[1]])
-        gradient(half + 64, half + quarter)
         gradient(half + quarter, SLOTS)
         quantise_gradient(half, half + quarter)
         quantise_gradient(half + quarter, SLOTS)

@@ -22,10 +22,12 @@ P = 128
 LANES = 4
 BANK = 512
 RUN = 4
-GRAIN = 256
+GRAIN = 128
 GRAINS = DOCS // GRAIN
-GROUPS = [(0, 1), (1, 2), (2, 4), (4, 6), (6, 7), (7, 8)]
+PER_BANK = BANK // GRAIN
+GROUPS = [(0, 1), (1, 2), (2, 4), (4, 8), (8, 12), (12, 13), (13, 15), (15, 16)]
 SCALAR_WEAVES = 2
+STORES = {4: 0, 8: 4, 12: 8, 15: 12, 16: 15}
 
 
 def tile_attend_grag_d_pl_kernel(tc, xT, dT, us, ts, lk, wt, offs, out_0, out_1, out_2):
@@ -118,7 +120,7 @@ def tile_attend_grag_d_pl_kernel(tc, xT, dT, us, ts, lk, wt, offs, out_0, out_1,
             nc.tensor.matmul_mx(out=acc, lhsT=xd_codes[:, cols].bitcast(E4M3X4), lhsT_scale=xd_scales[:, cols],
                                 rhs=dg_codes[:, slots].bitcast(E4M3X4), rhs_scale=dg_scales[:, slots], start=True, stop=True)
 
-        pieces = [(j, halves[h]) for h in range(2) for j in range(2)] + [(j, slice(0, SLOTS)) for j in range(2, LANES)]
+        pieces = [(0, halves[h]) for h in range(2)] + [(j, slice(0, SLOTS)) for j in range(1, LANES)]
         scores = [bank(b, "scores%d" % b) for b in range(len(pieces))]
         for b, (j, slots) in enumerate(pieces):
             score(scores[b][:, slots], j, slots)
@@ -142,38 +144,45 @@ def tile_attend_grag_d_pl_kernel(tc, xT, dT, us, ts, lk, wt, offs, out_0, out_1,
 
         def lik_sum(j):
             c = 2 * (j % 2) + 1
-            nc.vector.scalar_tensor_tensor(et[:, j, :], e[j][:], -1.0, lk_sb[:, j, :], ALU.mult, ALU.mult, accum_out=sums[j // 2][:, c : c + 1])
+            nc.vector.scalar_tensor_tensor(z[j][:], e[j][:], -1.0, lk_sb[:, j, :], ALU.mult, ALU.mult, accum_out=sums[j // 2][:, c : c + 1])
 
-        def factors(h):
+        def factors(h, parts):
             nc.vector.reciprocal(inv[h][:], sums[h][:])
-            for j in (2 * h, 2 * h + 1):
-                c = 2 * (j % 2)
-                nc.scalar.activation(hh[:, j, :], lk_sb[:, j, :], ACT.Identity, bias=inv[h][:, c : c + 1], scale=inv[h][:, c + 1 : c + 2])
+            for slots in parts:
+                for j in (2 * h, 2 * h + 1):
+                    c = 2 * (j % 2)
+                    nc.scalar.activation(hh[:, j, slots], lk_sb[:, j, slots], ACT.Identity, bias=inv[h][:, c : c + 1], scale=inv[h][:, c + 1 : c + 2])
 
-        def scaled_e(j):
-            nc.vector.scalar_tensor_tensor(et[:, j, :], e[j][:], wu[:, j : j + 1], ts_g[:], ALU.mult, ALU.mult)
+        def scaled_e(j, slots):
+            nc.vector.scalar_tensor_tensor(et[:, j, slots], e[j][:, slots], wu[:, j : j + 1], ts_g[:, slots], ALU.mult, ALU.mult)
 
-        for b in range(4):
+        tsw = [sb.tile([P, SLOTS], F32, name="tsw%d" % j, tag="tsw%d" % j) for j in range(2)]
+        for j in range(2):
+            nc.scalar.activation(tsw[j][:], ts_g[:], ACT.Copy, scale=wu[:, j : j + 1])
+
+        for b in range(3):
             scale_scores(b)
         row_max(0)
+        nc.gpsimd.tensor_tensor(et[:, 0, :], e[0][:], tsw[0][:], ALU.mult)
+        scale_scores(3)
         row_max(1)
+        nc.gpsimd.tensor_tensor(et[:, 1, halves[0]], e[1][:, halves[0]], tsw[1][:, halves[0]], ALU.mult)
         scale_scores(4)
-        scale_scores(5)
         row_max(2)
         row_max(3)
-        for j in range(2):
-            windows.append(sb.tile([P, DOCS], F32, name="window%d" % (2 + j), tag="z%d" % j))
-            nc.gpsimd.memset(windows[2 + j][:], 0.0)
         lik_sum(0)
         lik_sum(1)
+        for j, tag in ((2, "tsw1"), (3, "z0")):
+            windows.append(sb.tile([P, DOCS], F32, name="window%d" % j, tag=tag))
+            nc.gpsimd.memset(windows[j][:], 0.0)
         lik_sum(2)
-        factors(0)
+        factors(0, [slice(0, SLOTS)])
         lik_sum(3)
-        scaled_e(0)
-        factors(1)
-        scaled_e(1)
-        scaled_e(2)
-        scaled_e(3)
+        scaled_e(2, halves[0])
+        factors(1, halves)
+        scaled_e(3, halves[0])
+        scaled_e(1, halves[1])
+        scaled_e(2, halves[1])
 
         g = sb.tile([P, SLOTS * LANES], BF16, name="g", align_bytes=64)
         g_codes = sb.tile([P, half + SLOTS], U32, name="g_codes", align_bytes=64)
@@ -199,11 +208,12 @@ def tile_attend_grag_d_pl_kernel(tc, xT, dT, us, ts, lk, wt, offs, out_0, out_1,
         dd = [sb.tile([P, SLOTS], F32, name="dd%d" % j) for j in range(LANES)]
         quarter = SLOTS // 4
         gradient(0, half)
-        gradient(half, half + quarter)
+        scaled_e(3, halves[1])
         quantise_gradient(0, half)
         early = bank(0, "early")
         table_gradient(early, 0, 0)
         nc.scalar.copy(out=dd[0][:, halves[0]], in_=early[:, halves[1]])
+        gradient(half, half + quarter)
         gradient(half + quarter, SLOTS)
         quantise_gradient(half, half + quarter)
         quantise_gradient(half + quarter, SLOTS)
@@ -228,7 +238,7 @@ def tile_attend_grag_d_pl_kernel(tc, xT, dT, us, ts, lk, wt, offs, out_0, out_1,
             else:
                 nc.vector.tensor_copy(windows[j][:].indirect(offsets[:]), dd[j][:])
             nc.sync.dma_start(out=out_rows[:, j, :], in_=windows[j][:])
-            for k0, k1 in (GROUPS if j == LANES - 1 else [(0, GRAINS)]):
+            for k0, k1 in (GROUPS[:5] + [(12, GRAINS)] if j == LANES - 1 else [(0, GRAINS)]):
                 round_lane(j, k0, k1)
 
         words_out = out_1.rearrange("a p c l -> p (a c l)").bitcast(I32)
@@ -252,10 +262,10 @@ def tile_attend_grag_d_pl_kernel(tc, xT, dT, us, ts, lk, wt, offs, out_0, out_1,
         def quantise(n):
             k0, k1 = GROUPS[n]
             cols = slice(GRAIN * k0, GRAIN * k1)
-            nc.vector.quantize_mx(out=y_codes[:, cols].bitcast(E4M3X4), scales=y_scales[4 * (k0 // 2) : P, GRAIN * (k0 % 2) : GRAIN * (k0 % 2 + k1 - k0)],
+            nc.vector.quantize_mx(out=y_codes[:, cols].bitcast(E4M3X4), scales=y_scales[4 * (k0 // PER_BANK) : P, GRAIN * (k0 % PER_BANK) : GRAIN * (k0 % PER_BANK + k1 - k0)],
                                   in_=woven[:, GRAIN * LANES * k0 : GRAIN * LANES * k1])
-            if n > 0:
-                first = 0 if n == 1 else GRAIN * k0
+            if k1 in STORES:
+                first = GRAIN * STORES[k1]
                 nc.sync.dma_start(out=words_out[:, first : GRAIN * k1], in_=y_codes[:, first : GRAIN * k1].bitcast(I32))
 
         weave(0)

@@ -60,8 +60,8 @@ def tile_attend_grag_d_pl_kernel(tc, xT, dT, us, ts, lk, wt, offs, out_0, out_1,
         ident = sb.tile([P, P], F32, name="ident")
         make_identity(nc, ident[:])
 
-        windows = [sb.tile([P, DOCS], F32, name="window%d" % j) for j in range(2)]
-        for j in range(2):
+        windows = [sb.tile([P, DOCS], F32, name="window%d" % j) for j in range(LANES)]
+        for j in range(LANES):
             nc.vector.memset(windows[j][:].bitcast(I32), 0)
 
         ts_all = sb.tile([P, DOCS], F32, name="ts_all")
@@ -73,12 +73,12 @@ def tile_attend_grag_d_pl_kernel(tc, xT, dT, us, ts, lk, wt, offs, out_0, out_1,
                 col = RUN * b + m
                 nc.tensor.transpose(spread[:, P * m : P * (m + 1)], ts_cols[:, col : col + 1].to_broadcast([P, P]), ident[:])
             nc.scalar.copy(out=ts_view[:, :, RUN * b : RUN * (b + 1)], in_=spread[:].rearrange("q (m p) -> q p m", m=RUN))
-        ts_g = sb.tile([P, SLOTS], F32, name="ts_g")
-        nc.vector.tensor_copy(ts_g[:], ts_all[:].indirect(offsets[:]))
 
         xd = sb.tile([P, R * LANES], BF16, name="xd", align_bytes=64)
         nc.vector.tensor_copy(out=xd[:].rearrange("p (j s t) -> p s t j", j=LANES, t=LANES),
                               in_=x_raw[:].rearrange("p t (s j) -> p s t j", j=LANES))
+        ts_g = sb.tile([P, SLOTS], F32, name="ts_g")
+        nc.vector.tensor_copy(ts_g[:], ts_all[:].indirect(offsets[:]))
         xd_codes = sb.tile([P, R], U32, name="xd_codes", align_bytes=64)
         xd_scales = sb.tile([P, R], U8, name="xd_scales", align_bytes=64)
         nc.vector.quantize_mx(out=xd_codes[:].bitcast(E4M3X4), scales=xd_scales[:], in_=xd[:])
@@ -172,9 +172,6 @@ def tile_attend_grag_d_pl_kernel(tc, xT, dT, us, ts, lk, wt, offs, out_0, out_1,
         row_max(3)
         lik_sum(0)
         lik_sum(1)
-        for j, tag in ((2, "tsw1"), (3, "z0")):
-            windows.append(sb.tile([P, DOCS], F32, name="window%d" % j, tag=tag))
-            nc.gpsimd.memset(windows[j][:], 0.0)
         lik_sum(2)
         factors(0, [slice(0, SLOTS)])
         lik_sum(3)
@@ -223,8 +220,9 @@ def tile_attend_grag_d_pl_kernel(tc, xT, dT, us, ts, lk, wt, offs, out_0, out_1,
         pair_lanes = pairs[:].rearrange("p (k u c e) -> p k u c e", u=2, c=GRAIN, e=2)
 
         def round_lane(j, k0, k1):
-            nc.scalar.copy(out=pair_lanes[:, k0:k1, j // 2, :, j % 2],
-                           in_=windows[j][:, GRAIN * k0 : GRAIN * k1].rearrange("p (k c) -> p k c", c=GRAIN))
+            dst = pair_lanes[:, k0:k1, j // 2, :, j % 2]
+            src = windows[j][:, GRAIN * k0 : GRAIN * k1].rearrange("p (k c) -> p k c", c=GRAIN)
+            nc.scalar.copy(out=dst, in_=src)
 
         for j in range(LANES):
             acc = bank(LANES + j, "grad%d" % j)

@@ -156,17 +156,11 @@ def tile_attend_grag_d_pl_kernel(tc, xT, dT, us, ts, lk, wt, offs, out_0, out_1,
         def scaled_e(j, slots):
             nc.vector.scalar_tensor_tensor(et[:, j, slots], e[j][:, slots], wu[:, j : j + 1], ts_g[:, slots], ALU.mult, ALU.mult)
 
-        tsw = [sb.tile([P, SLOTS], F32, name="tsw%d" % j, tag="tsw%d" % j) for j in range(2)]
-        for j in range(2):
-            nc.scalar.activation(tsw[j][:], ts_g[:], ACT.Copy, scale=wu[:, j : j + 1])
-
         for b in range(3):
             scale_scores(b)
         row_max(0)
-        nc.gpsimd.tensor_tensor(et[:, 0, :], e[0][:], tsw[0][:], ALU.mult)
         scale_scores(3)
         row_max(1)
-        nc.gpsimd.tensor_tensor(et[:, 1, halves[0]], e[1][:, halves[0]], tsw[1][:, halves[0]], ALU.mult)
         scale_scores(4)
         row_max(2)
         row_max(3)
@@ -175,11 +169,11 @@ def tile_attend_grag_d_pl_kernel(tc, xT, dT, us, ts, lk, wt, offs, out_0, out_1,
         lik_sum(2)
         factors(0, [slice(0, SLOTS)])
         lik_sum(3)
-        scaled_e(2, halves[0])
+        scaled_e(0, slice(0, SLOTS))
         factors(1, halves)
+        scaled_e(1, slice(0, SLOTS))
+        scaled_e(2, slice(0, SLOTS))
         scaled_e(3, halves[0])
-        scaled_e(1, halves[1])
-        scaled_e(2, halves[1])
 
         g = sb.tile([P, SLOTS * LANES], BF16, name="g", align_bytes=64)
         g_codes = sb.tile([P, half + SLOTS], U32, name="g_codes", align_bytes=64)
@@ -250,8 +244,8 @@ def tile_attend_grag_d_pl_kernel(tc, xT, dT, us, ts, lk, wt, offs, out_0, out_1,
             span = slice(GRAIN * LANES * k0, GRAIN * LANES * k1)
             on_scalar = n >= len(GROUPS) - SCALAR_WEAVES
             word = U32 if on_scalar else I32
-            dst = woven[:, span].bitcast(word).rearrange("p (k c i u) -> p k c u i", c=GRAIN // RUN, i=RUN, u=2)
-            src = pairs[:, span].bitcast(word).rearrange("p (k u c i) -> p k c u i", c=GRAIN // RUN, i=RUN, u=2)
+            dst = woven[:, span].bitcast(word).rearrange("p (k c u) -> p k c u", c=GRAIN, u=2)
+            src = pairs[:, span].bitcast(word).rearrange("p (k u c) -> p k c u", c=GRAIN, u=2)
             if on_scalar:
                 nc.scalar.copy(out=dst, in_=src)
             else:

@@ -25,9 +25,10 @@ RUN = 4
 GRAIN = 128
 GRAINS = DOCS // GRAIN
 PER_BANK = BANK // GRAIN
-GROUPS = [(0, 1), (1, 2), (2, 4), (4, 8), (8, 12), (12, 13), (13, 15), (15, 16)]
+GROUPS = [(0, 1), (1, 2), (2, 4), (4, 6), (6, 8), (8, 10), (10, 12), (12, 13), (13, 15), (15, 16)]
 SCALAR_WEAVES = 2
 STORES = {4: 0, 8: 4, 12: 8, 15: 12, 16: 15}
+LATE = 14
 
 
 def tile_attend_grag_d_pl_kernel(tc, xT, dT, us, ts, lk, wt, offs, out_0, out_1, out_2):
@@ -230,8 +231,15 @@ def tile_attend_grag_d_pl_kernel(tc, xT, dT, us, ts, lk, wt, offs, out_0, out_1,
             else:
                 nc.vector.tensor_copy(windows[j][:].indirect(offsets[:]), dd[j][:])
             nc.sync.dma_start(out=out_rows[:, j, :], in_=windows[j][:])
-            for k0, k1 in (GROUPS[:5] + [(12, GRAINS)] if j == LANES - 1 else [(0, GRAINS)]):
-                round_lane(j, k0, k1)
+            if j < LANES - 2:
+                round_lane(j, 0, GRAINS)
+            elif j == LANES - 2:
+                round_lane(j, 0, LATE)
+            else:
+                for k0, k1 in GROUPS[:-SCALAR_WEAVES]:
+                    round_lane(j, k0, k1)
+                round_lane(j - 1, LATE, GRAINS)
+                round_lane(j, GROUPS[-SCALAR_WEAVES][0], GRAINS)
 
         words_out = out_1.rearrange("a p c l -> p (a c l)").bitcast(I32)
         scales_out = out_2.rearrange("o f (a c) -> a (o f) c", c=BANK).bitcast(I32)

@@ -147,15 +147,21 @@ def tile_attend_grag_d_pl_kernel(tc, xT, dT, us, ts, lk, wt, offs, out_0, out_1,
             c = 2 * (j % 2) + 1
             nc.vector.scalar_tensor_tensor(z[j][:], e[j][:], -1.0, lk_sb[:, j, :], ALU.mult, ALU.mult, accum_out=sums[j // 2][:, c : c + 1])
 
-        def factors(h, parts):
+        weighted = [sb.tile([P, 4], F32, name="weighted%d" % h) for h in range(2)]
+
+        def invert(h):
             nc.vector.reciprocal(inv[h][:], sums[h][:])
+
+        def factors(h, parts):
+            nc.vector.tensor_tensor(weighted[h][:].rearrange("p (j c) -> p j c", c=2), inv[h][:].rearrange("p (j c) -> p j c", c=2),
+                                    wu[:, 2 * h : 2 * h + 2].unsqueeze(2).to_broadcast([P, 2, 2]), ALU.mult)
             for slots in parts:
                 for j in (2 * h, 2 * h + 1):
                     c = 2 * (j % 2)
-                    nc.scalar.activation(hh[:, j, slots], lk_sb[:, j, slots], ACT.Identity, bias=inv[h][:, c : c + 1], scale=inv[h][:, c + 1 : c + 2])
+                    nc.scalar.activation(hh[:, j, slots], lk_sb[:, j, slots], ACT.Identity, bias=weighted[h][:, c : c + 1], scale=weighted[h][:, c + 1 : c + 2])
 
         def scaled_e(j, slots):
-            nc.vector.scalar_tensor_tensor(et[:, j, slots], e[j][:, slots], wu[:, j : j + 1], ts_g[:, slots], ALU.mult, ALU.mult)
+            nc.vector.tensor_tensor(et[:, j, slots], e[j][:, slots], ts_g[:, slots], ALU.mult)
 
         for b in range(3):
             scale_scores(b)
@@ -167,12 +173,16 @@ def tile_attend_grag_d_pl_kernel(tc, xT, dT, us, ts, lk, wt, offs, out_0, out_1,
         row_max(3)
         lik_sum(0)
         lik_sum(1)
+        scaled_e(0, halves[0])
+        invert(0)
         lik_sum(2)
         factors(0, [slice(0, SLOTS)])
         lik_sum(3)
-        scaled_e(0, slice(0, SLOTS))
+        scaled_e(0, halves[1])
+        invert(1)
+        scaled_e(1, halves[0])
         factors(1, halves)
-        scaled_e(1, slice(0, SLOTS))
+        scaled_e(1, halves[1])
         scaled_e(2, slice(0, SLOTS))
         scaled_e(3, halves[0])
 

@@ -61,11 +61,11 @@ def tile_attend_grag_d_pl_kernel(tc, xT, dT, us, ts, lk, wt, offs, out_0, out_1,
         ident = sb.tile([P, P], F32, name="ident")
         make_identity(nc, ident[:])
 
-        windows = [sb.tile([P, DOCS], F32, name="window%d" % j) for j in range(LANES)]
-        for j in range(LANES):
+        windows = [sb.tile([P, DOCS], F32, name="window%d" % j) for j in range(2)]
+        for j in range(2):
             nc.vector.memset(windows[j][:].bitcast(I32), 0)
 
-        ts_all = sb.tile([P, DOCS], F32, name="ts_all")
+        ts_all = sb.tile([P, DOCS], F32, name="ts_all", tag="ts_all")
         per = DOCS // P
         ts_view = ts_all[:].rearrange("q (p m) -> q p m", m=per)
         for b in range(per // RUN):
@@ -78,11 +78,12 @@ def tile_attend_grag_d_pl_kernel(tc, xT, dT, us, ts, lk, wt, offs, out_0, out_1,
         xd = sb.tile([P, R * LANES], BF16, name="xd", align_bytes=64)
         nc.vector.tensor_copy(out=xd[:].rearrange("p (j s t) -> p s t j", j=LANES, t=LANES),
                               in_=x_raw[:].rearrange("p t (s j) -> p s t j", j=LANES))
-        ts_g = sb.tile([P, SLOTS], F32, name="ts_g")
-        nc.vector.tensor_copy(ts_g[:], ts_all[:].indirect(offsets[:]))
         xd_codes = sb.tile([P, R], U32, name="xd_codes", align_bytes=64)
         xd_scales = sb.tile([P, R], U8, name="xd_scales", align_bytes=64)
         nc.vector.quantize_mx(out=xd_codes[:].bitcast(E4M3X4), scales=xd_scales[:], in_=xd[:])
+
+        ts_g = sb.tile([P, SLOTS], F32, name="ts_g")
+        nc.vector.tensor_copy(ts_g[:], ts_all[:].indirect(offsets[:]))
 
         xd_words = xd[:].bitcast(F32).rearrange("p (j s u) -> p j s u", j=LANES, u=2)
         xr = sb.tile([P, D * LANES], BF16, name="xr", align_bytes=64)
@@ -98,19 +99,24 @@ def tile_attend_grag_d_pl_kernel(tc, xT, dT, us, ts, lk, wt, offs, out_0, out_1,
 
         half = SLOTS // 2
         halves = [slice(half * h, half * (h + 1)) for h in range(2)]
-        dg = sb.tile([P, SLOTS * LANES], BF16, name="dg", align_bytes=64)
-        dg_lanes = dg[:].rearrange("p (i t) -> p i t", t=LANES)
-        dg_flat = sb.tile([P, 2 * SLOTS], BF16, name="dg_flat")
+        g_codes = sb.tile([P, half + SLOTS], U32, name="g_codes", align_bytes=64)
+        g_scales = sb.tile([P, half + SLOTS], U8, name="g_scales", align_bytes=64)
+        nc.gpsimd.memset(g_codes[:, 0:half], 0)
+        nc.gpsimd.memset(g_scales[:, 0:half], 0)
+        dg_flat = sb.tile([P, 2 * SLOTS], BF16, name="dg_flat", tag="ts_all")
         for t in range(2):
             nc.vector.tensor_copy(dg_flat[:, SLOTS * t : SLOTS * (t + 1)], docs[t][:].indirect(offsets[:]))
-        nc.scalar.copy(out=dg_lanes[:, :, 0:2], in_=dg_flat[:].rearrange("p (t i) -> p i t", t=2))
-        xr_codes = sb.tile([P, D], U32, name="xr_codes", tag="docs1", align_bytes=64)
+        xr_codes = sb.tile([P, D], U32, name="xr_codes", tag="docs0", align_bytes=64)
         xr_scales = sb.tile([P, D], U8, name="xr_scales", align_bytes=64)
         nc.vector.quantize_mx(out=xr_codes[:].bitcast(E4M3X4), scales=xr_scales[:], in_=xr[:])
+        dg = sb.tile([P, SLOTS * LANES], BF16, name="dg", tag="docs1", align_bytes=64)
+        dg_lanes = dg[:].rearrange("p (i t) -> p i t", t=LANES)
+        for h in range(2):
+            nc.scalar.copy(out=dg_lanes[:, halves[h], 0:2], in_=dg_flat[:].rearrange("p (t i) -> p i t", t=2)[:, halves[h], :])
         nc.vector.tensor_copy(dg_lanes[:, :, LANES - 2], docs[LANES - 2][:].indirect(offsets[:]))
         for h in range(2):
             nc.vector.tensor_copy(dg_lanes[:, halves[h], LANES - 1], docs[LANES - 1][:].indirect(offsets[:, 16 * h : 16 * (h + 1)]))
-        dg_codes = sb.tile([P, SLOTS], U32, name="dg_codes", align_bytes=64)
+        dg_codes = sb.tile([P, SLOTS], U32, name="dg_codes", tag="dg_codes", align_bytes=64)
         dg_scales = sb.tile([P, SLOTS], U8, name="dg_scales", align_bytes=64)
         for h in range(2):
             nc.vector.quantize_mx(out=dg_codes[:, halves[h]].bitcast(E4M3X4), scales=dg_scales[:, halves[h]],
@@ -125,6 +131,10 @@ def tile_attend_grag_d_pl_kernel(tc, xT, dT, us, ts, lk, wt, offs, out_0, out_1,
         scores = [bank(b, "scores%d" % b) for b in range(len(pieces))]
         for b, (j, slots) in enumerate(pieces):
             score(scores[b][:, slots], j, slots)
+
+        for j, tag in ((2, "docs1"), (3, "dg_codes")):
+            windows.append(sb.tile([P, DOCS], F32, name="window%d" % j, tag=tag, align_bytes=64))
+            nc.gpsimd.memset(windows[j][:].bitcast(I32), 0)
 
         z = [sb.tile([P, SLOTS], F32, name="z%d" % j, tag="z%d" % j) for j in range(LANES)]
         e = [sb.tile([P, SLOTS], F32, name="e%d" % j) for j in range(LANES)]
@@ -187,10 +197,6 @@ def tile_attend_grag_d_pl_kernel(tc, xT, dT, us, ts, lk, wt, offs, out_0, out_1,
         scaled_e(3, halves[0])
 
         g = sb.tile([P, SLOTS * LANES], BF16, name="g", align_bytes=64)
-        g_codes = sb.tile([P, half + SLOTS], U32, name="g_codes", align_bytes=64)
-        g_scales = sb.tile([P, half + SLOTS], U8, name="g_scales", align_bytes=64)
-        nc.gpsimd.memset(g_codes[:, 0:half], 0)
-        nc.gpsimd.memset(g_scales[:, 0:half], 0)
 
         def gradient(i0, i1):
             nc.vector.tensor_tensor(g[:, LANES * i0 : LANES * i1].rearrange("p (c i j) -> p c j i", i=RUN, j=LANES),

@@ -113,6 +113,11 @@ def tile_attend_grag_d_pl_kernel(tc, xT, dT, us, ts, lk, wt, offs, out_0, out_1,
         dg_lanes = dg[:].rearrange("p (i t) -> p i t", t=LANES)
         for h in range(2):
             nc.scalar.copy(out=dg_lanes[:, halves[h], 0:2], in_=dg_flat[:].rearrange("p (t i) -> p i t", t=2)[:, halves[h], :])
+        ts_turned = bank(6, "ts_turned")
+        for q in range(2, LANES):
+            nc.tensor.transpose(ts_turned[:, P * q : P * (q + 1)], ts_g[:, P * q : P * (q + 1)], ident[:])
+        ts_slot = sb.tile([P, 2], F32, name="ts_slot")
+        nc.scalar.copy(out=ts_slot[:], in_=ts_turned[:, 2 * P : BANK : P])
         nc.vector.tensor_copy(dg_lanes[:, :, LANES - 2], docs[LANES - 2][:].indirect(offsets[:]))
         for h in range(2):
             nc.vector.tensor_copy(dg_lanes[:, halves[h], LANES - 1], docs[LANES - 1][:].indirect(offsets[:, 16 * h : 16 * (h + 1)]))
@@ -137,11 +142,11 @@ def tile_attend_grag_d_pl_kernel(tc, xT, dT, us, ts, lk, wt, offs, out_0, out_1,
             nc.gpsimd.memset(windows[j][:].bitcast(I32), 0)
 
         z = [sb.tile([P, SLOTS], F32, name="z%d" % j, tag="z%d" % j) for j in range(LANES)]
-        e = [sb.tile([P, SLOTS], F32, name="e%d" % j) for j in range(LANES)]
+        e = sb.tile([P, LANES, SLOTS], F32, name="e")
         neg_max = [sb.tile([P, 1], F32, name="neg_max%d" % j) for j in range(LANES)]
         sums = [sb.tile([P, 4], F32, name="sums%d" % h) for h in range(2)]
         inv = [sb.tile([P, 4], F32, name="inv%d" % h) for h in range(2)]
-        et = sb.tile([P, LANES, SLOTS], F32, name="et")
+        et = sb.tile([P, LANES, SLOTS // 2], F32, name="et")
         hh = sb.tile([P, LANES, SLOTS], F32, name="hh")
 
         def scale_scores(b):
@@ -151,27 +156,41 @@ def tile_attend_grag_d_pl_kernel(tc, xT, dT, us, ts, lk, wt, offs, out_0, out_1,
         def row_max(j):
             nc.vector.tensor_reduce(neg_max[j][:], z[j][:], AX.X, ALU.max, negate=True)
             c = 2 * (j % 2)
-            nc.scalar.activation(e[j][:], z[j][:], ACT.Exp, bias=neg_max[j][:], scale=1.0, accum_out=sums[j // 2][:, c : c + 1])
+            nc.scalar.activation(e[:, j, :], z[j][:], ACT.Exp, bias=neg_max[j][:], scale=1.0, accum_out=sums[j // 2][:, c : c + 1])
 
         def lik_sum(j):
             c = 2 * (j % 2) + 1
-            nc.vector.scalar_tensor_tensor(z[j][:], e[j][:], -1.0, lk_sb[:, j, :], ALU.mult, ALU.mult, accum_out=sums[j // 2][:, c : c + 1])
+            nc.vector.scalar_tensor_tensor(z[j][:], e[:, j, :], -1.0, lk_sb[:, j, :], ALU.mult, ALU.mult, accum_out=sums[j // 2][:, c : c + 1])
 
         weighted = [sb.tile([P, 4], F32, name="weighted%d" % h) for h in range(2)]
 
         def invert(h):
             nc.vector.reciprocal(inv[h][:], sums[h][:])
 
-        def factors(h, parts):
+        def weigh(h):
             nc.vector.tensor_tensor(weighted[h][:].rearrange("p (j c) -> p j c", c=2), inv[h][:].rearrange("p (j c) -> p j c", c=2),
                                     wu[:, 2 * h : 2 * h + 2].unsqueeze(2).to_broadcast([P, 2, 2]), ALU.mult)
-            for slots in parts:
-                for j in (2 * h, 2 * h + 1):
-                    c = 2 * (j % 2)
-                    nc.scalar.activation(hh[:, j, slots], lk_sb[:, j, slots], ACT.Identity, bias=weighted[h][:, c : c + 1], scale=weighted[h][:, c + 1 : c + 2])
 
-        def scaled_e(j, slots):
-            nc.vector.tensor_tensor(et[:, j, slots], e[j][:, slots], ts_g[:, slots], ALU.mult)
+        def factors(h, slots):
+            for j in (2 * h, 2 * h + 1):
+                c = 2 * (j % 2)
+                nc.scalar.activation(hh[:, j, slots], lk_sb[:, j, slots], ACT.Identity, bias=weighted[h][:, c : c + 1], scale=weighted[h][:, c + 1 : c + 2])
+
+        quarters = [slice(P * q, P * (q + 1)) for q in range(LANES)]
+
+        def scaled_e(q):
+            nc.vector.tensor_tensor(et[:, :, quarters[q]], e[:, :, quarters[q]], ts_g[:, quarters[q]].unsqueeze(1).to_broadcast([P, LANES, P]), ALU.mult)
+
+        def turned_product(q):
+            there = bank(3 + q, "e_by_slot%d" % q)
+            for j in range(LANES):
+                nc.tensor.transpose(there[:, quarters[j]], e[:, j, quarters[q]], ident[:])
+            scaled = sb.tile([P, BANK], F32, name="et_by_slot%d" % q)
+            nc.scalar.activation(scaled[:], there[:], ACT.Copy, scale=ts_slot[:, q - 2 : q - 1])
+            back = bank((7, 1)[q - 2], "et_by_question%d" % q)
+            for j in range(LANES):
+                nc.tensor.transpose(back[:, quarters[j]], scaled[:, quarters[j]], ident[:])
+            return back[:].rearrange("p (j i) -> p j i", j=LANES)
 
         for b in range(3):
             scale_scores(b)
@@ -183,25 +202,29 @@ def tile_attend_grag_d_pl_kernel(tc, xT, dT, us, ts, lk, wt, offs, out_0, out_1,
         row_max(3)
         lik_sum(0)
         lik_sum(1)
-        scaled_e(0, halves[0])
-        invert(0)
         lik_sum(2)
-        factors(0, [slice(0, SLOTS)])
+        invert(0)
         lik_sum(3)
-        scaled_e(0, halves[1])
+        weigh(0)
         invert(1)
-        scaled_e(1, halves[0])
-        factors(1, halves)
-        scaled_e(1, halves[1])
-        scaled_e(2, slice(0, SLOTS))
-        scaled_e(3, halves[0])
+        products = [et[:, :, quarters[0]], et[:, :, quarters[1]], turned_product(2)]
+        factors(0, halves[0])
+        scaled_e(0)
+        weigh(1)
+        factors(1, quarters[0])
+        scaled_e(1)
+        factors(1, quarters[1])
+        products.append(turned_product(3))
+        for q in range(2, LANES):
+            factors(0, quarters[q])
+            factors(1, quarters[q])
 
         g = sb.tile([P, SLOTS * LANES], BF16, name="g", align_bytes=64)
 
-        def gradient(i0, i1):
-            nc.vector.tensor_tensor(g[:, LANES * i0 : LANES * i1].rearrange("p (c i j) -> p c j i", i=RUN, j=LANES),
-                                    et[:, :, i0:i1].rearrange("p j (c i) -> p c j i", i=RUN),
-                                    hh[:, :, i0:i1].rearrange("p j (c i) -> p c j i", i=RUN), ALU.mult)
+        def gradient(q):
+            nc.vector.tensor_tensor(g[:, BANK * q : BANK * (q + 1)].rearrange("p (c i j) -> p c j i", i=RUN, j=LANES),
+                                    products[q].rearrange("p j (c i) -> p c j i", i=RUN),
+                                    hh[:, :, quarters[q]].rearrange("p j (c i) -> p c j i", i=RUN), ALU.mult)
 
         def quantise_gradient(i0, i1):
             nc.vector.quantize_mx(out=g_codes[:, half + i0 : half + i1].bitcast(E5M2X4), scales=g_scales[:, half + i0 : half + i1],
@@ -215,14 +238,14 @@ def tile_attend_grag_d_pl_kernel(tc, xT, dT, us, ts, lk, wt, offs, out_0, out_1,
 
         dd = [sb.tile([P, SLOTS], F32, name="dd%d" % j) for j in range(LANES)]
         quarter = SLOTS // 4
-        gradient(0, half)
-        scaled_e(3, halves[1])
+        gradient(0)
+        gradient(1)
+        gradient(2)
         quantise_gradient(0, half)
         early = bank(0, "early")
         table_gradient(early, 0, 0)
         nc.scalar.copy(out=dd[0][:, halves[0]], in_=early[:, halves[1]])
-        gradient(half, half + quarter)
-        gradient(half + quarter, SLOTS)
+        gradient(3)
         quantise_gradient(half, half + quarter)
         quantise_gradient(half + quarter, SLOTS)
 
@@ -236,7 +259,7 @@ def tile_attend_grag_d_pl_kernel(tc, xT, dT, us, ts, lk, wt, offs, out_0, out_1,
             nc.scalar.copy(out=dst, in_=src)
 
         for j in range(LANES):
-            acc = bank(LANES + j, "grad%d" % j)
+            acc = bank(2 + j, "grad%d" % j)
             table_gradient(acc, j, half)
             todo = halves[1] if j == 0 else slice(0, SLOTS)
             nc.scalar.copy(out=dd[j][:, todo], in_=acc[:, todo])

@@ -144,8 +144,14 @@ def tile_attend_grag_d_pl_kernel(tc, xT, dT, us, ts, lk, wt, offs, out_0, out_1,
         z = [sb.tile([P, SLOTS], F32, name="z%d" % j, tag="z%d" % j) for j in range(LANES)]
         e = sb.tile([P, LANES, SLOTS], F32, name="e")
         neg_max = [sb.tile([P, 1], F32, name="neg_max%d" % j) for j in range(LANES)]
-        sums = [sb.tile([P, 4], F32, name="sums%d" % h) for h in range(2)]
-        inv = [sb.tile([P, 4], F32, name="inv%d" % h) for h in range(2)]
+        t1 = sb.tile([P, LANES], F32, name="t1")
+        t1_inv = sb.tile([P, LANES], F32, name="t1_inv")
+        h_bias = sb.tile([P, LANES], F32, name="h_bias")
+        t2 = [sb.tile([P, 2], F32, name="t2_%d" % h) for h in range(2)]
+        h_scale = [sb.tile([P, 2], F32, name="h_scale%d" % h) for h in range(2)]
+        lkw = sb.tile([P, LANES, SLOTS], F32, name="lkw")
+        for j in range(LANES):
+            nc.scalar.activation(lkw[:, j, :], lk_sb[:, j, :], ACT.Copy, scale=wu[:, j : j + 1])
         et = sb.tile([P, LANES, SLOTS // 2], F32, name="et")
         hh = sb.tile([P, LANES, SLOTS], F32, name="hh")
 
@@ -155,26 +161,15 @@ def tile_attend_grag_d_pl_kernel(tc, xT, dT, us, ts, lk, wt, offs, out_0, out_1,
 
         def row_max(j):
             nc.vector.tensor_reduce(neg_max[j][:], z[j][:], AX.X, ALU.max, negate=True)
-            c = 2 * (j % 2)
-            nc.scalar.activation(e[:, j, :], z[j][:], ACT.Exp, bias=neg_max[j][:], scale=1.0, accum_out=sums[j // 2][:, c : c + 1])
+            nc.scalar.activation(e[:, j, :], z[j][:], ACT.Exp, bias=neg_max[j][:], scale=1.0, accum_out=t1[:, j : j + 1])
 
         def lik_sum(j):
-            c = 2 * (j % 2) + 1
-            nc.vector.scalar_tensor_tensor(z[j][:], e[:, j, :], -1.0, lk_sb[:, j, :], ALU.mult, ALU.mult, accum_out=sums[j // 2][:, c : c + 1])
-
-        weighted = [sb.tile([P, 4], F32, name="weighted%d" % h) for h in range(2)]
-
-        def invert(h):
-            nc.vector.reciprocal(inv[h][:], sums[h][:])
-
-        def weigh(h):
-            nc.vector.tensor_tensor(weighted[h][:].rearrange("p (j c) -> p j c", c=2), inv[h][:].rearrange("p (j c) -> p j c", c=2),
-                                    wu[:, 2 * h : 2 * h + 2].unsqueeze(2).to_broadcast([P, 2, 2]), ALU.mult)
+            nc.vector.scalar_tensor_tensor(z[j][:], e[:, j, :], -1.0, lk_sb[:, j, :], ALU.mult, ALU.mult, accum_out=t2[j // 2][:, j % 2 : j % 2 + 1])
 
         def factors(h, slots):
-            for j in (2 * h, 2 * h + 1):
-                c = 2 * (j % 2)
-                nc.scalar.activation(hh[:, j, slots], lk_sb[:, j, slots], ACT.Identity, bias=weighted[h][:, c : c + 1], scale=weighted[h][:, c + 1 : c + 2])
+            for c in range(2):
+                j = 2 * h + c
+                nc.scalar.activation(hh[:, j, slots], lkw[:, j, slots], ACT.Identity, bias=h_bias[:, j : j + 1], scale=h_scale[h][:, c : c + 1])
 
         quarters = [slice(P * q, P * (q + 1)) for q in range(LANES)]
 
@@ -202,22 +197,23 @@ def tile_attend_grag_d_pl_kernel(tc, xT, dT, us, ts, lk, wt, offs, out_0, out_1,
         row_max(3)
         lik_sum(0)
         lik_sum(1)
-        lik_sum(2)
-        invert(0)
-        lik_sum(3)
-        weigh(0)
-        invert(1)
-        products = [et[:, :, quarters[0]], et[:, :, quarters[1]], turned_product(2)]
+        nc.vector.reciprocal(t1_inv[:], t1[:])
+        nc.vector.reciprocal(h_scale[0][:], t2[0][:])
+        nc.vector.tensor_tensor(h_bias[:], t1_inv[:], wu[:], ALU.mult)
         factors(0, halves[0])
+        lik_sum(2)
+        lik_sum(3)
+        products = [et[:, :, quarters[0]], et[:, :, quarters[1]], turned_product(2)]
+        factors(0, quarters[2])
         scaled_e(0)
-        weigh(1)
-        factors(1, quarters[0])
+        nc.vector.reciprocal(h_scale[1][:], t2[1][:])
         scaled_e(1)
+        factors(1, quarters[0])
         factors(1, quarters[1])
         products.append(turned_product(3))
-        for q in range(2, LANES):
-            factors(0, quarters[q])
-            factors(1, quarters[q])
+        factors(1, quarters[2])
+        factors(0, quarters[3])
+        factors(1, quarters[3])
 
         g = sb.tile([P, SLOTS * LANES], BF16, name="g", align_bytes=64)
 

@@ -114,10 +114,10 @@ def tile_attend_grag_d_pl_kernel(tc, xT, dT, us, ts, lk, wt, offs, out_0, out_1,
         for h in range(2):
             nc.scalar.copy(out=dg_lanes[:, halves[h], 0:2], in_=dg_flat[:].rearrange("p (t i) -> p i t", t=2)[:, halves[h], :])
         ts_turned = bank(6, "ts_turned")
-        for q in range(2, LANES):
+        for q in range(1, LANES):
             nc.tensor.transpose(ts_turned[:, P * q : P * (q + 1)], ts_g[:, P * q : P * (q + 1)], ident[:])
-        ts_slot = sb.tile([P, 2], F32, name="ts_slot")
-        nc.scalar.copy(out=ts_slot[:], in_=ts_turned[:, 2 * P : BANK : P])
+        ts_slot = sb.tile([P, LANES - 1], F32, name="ts_slot")
+        nc.scalar.copy(out=ts_slot[:], in_=ts_turned[:, P:BANK:P])
         nc.vector.tensor_copy(dg_lanes[:, :, LANES - 2], docs[LANES - 2][:].indirect(offsets[:]))
         for h in range(2):
             nc.vector.tensor_copy(dg_lanes[:, halves[h], LANES - 1], docs[LANES - 1][:].indirect(offsets[:, 16 * h : 16 * (h + 1)]))
@@ -143,7 +143,7 @@ def tile_attend_grag_d_pl_kernel(tc, xT, dT, us, ts, lk, wt, offs, out_0, out_1,
 
         z = [sb.tile([P, SLOTS], F32, name="z%d" % j, tag="z%d" % j) for j in range(LANES)]
         e = sb.tile([P, LANES, SLOTS], F32, name="e")
-        neg_max = [sb.tile([P, 1], F32, name="neg_max%d" % j) for j in range(LANES)]
+        neg_max = [sb.tile([P, 1], F32, name="neg_max%d" % j, tag="neg_max%d" % j) for j in range(LANES)]
         t1 = sb.tile([P, LANES], F32, name="t1")
         t1_inv = sb.tile([P, LANES], F32, name="t1_inv")
         h_bias = sb.tile([P, LANES], F32, name="h_bias")
@@ -152,8 +152,8 @@ def tile_attend_grag_d_pl_kernel(tc, xT, dT, us, ts, lk, wt, offs, out_0, out_1,
         lkw = sb.tile([P, LANES, SLOTS], F32, name="lkw")
         for j in range(LANES):
             nc.scalar.activation(lkw[:, j, :], lk_sb[:, j, :], ACT.Copy, scale=wu[:, j : j + 1])
-        et = sb.tile([P, LANES, SLOTS // 2], F32, name="et")
-        hh = sb.tile([P, LANES, SLOTS], F32, name="hh")
+        et = sb.tile([P, LANES, P], F32, name="et")
+        hh = sb.tile([P, LANES, SLOTS], F32, name="hh", tag="hh")
 
         def scale_scores(b):
             j, slots = pieces[b]
@@ -173,18 +173,25 @@ def tile_attend_grag_d_pl_kernel(tc, xT, dT, us, ts, lk, wt, offs, out_0, out_1,
 
         quarters = [slice(P * q, P * (q + 1)) for q in range(LANES)]
 
-        def scaled_e(q):
-            nc.vector.tensor_tensor(et[:, :, quarters[q]], e[:, :, quarters[q]], ts_g[:, quarters[q]].unsqueeze(1).to_broadcast([P, LANES, P]), ALU.mult)
+        def scaled_e(h):
+            tiles = slice(2 * h, 2 * h + 2)
+            nc.vector.tensor_tensor(et[:, tiles, :], e[:, tiles, quarters[0]], ts_g[:, quarters[0]].unsqueeze(1).to_broadcast([P, 2, P]), ALU.mult)
 
-        def turned_product(q):
-            there = bank(3 + q, "e_by_slot%d" % q)
+        def turn(h):
+            banks = [bank(3 + 2 * h + n, "e_by_slot%d_%d" % (h, n)) for n in range(2)]
+            places = [banks[(q - 1) // 2][:, halves[(q - 1) % 2]] for q in range(1, LANES)]
+            for c in range(2):
+                for q in range(1, LANES):
+                    nc.tensor.transpose(places[q - 1][:, quarters[c]], e[:, 2 * h + c, quarters[q]], ident[:])
+            return places
+
+        def scale_turned(h, q):
+            nc.scalar.activation(scaled[:, q - 1, halves[h]], by_slot[h][q - 1], ACT.Copy, scale=ts_slot[:, q - 1 : q])
+
+        def turn_back(q):
+            back = bank((7, 1, 2)[q - 1], "et_by_question%d" % q)
             for j in range(LANES):
-                nc.tensor.transpose(there[:, quarters[j]], e[:, j, quarters[q]], ident[:])
-            scaled = sb.tile([P, BANK], F32, name="et_by_slot%d" % q)
-            nc.scalar.activation(scaled[:], there[:], ACT.Copy, scale=ts_slot[:, q - 2 : q - 1])
-            back = bank((7, 1)[q - 2], "et_by_question%d" % q)
-            for j in range(LANES):
-                nc.tensor.transpose(back[:, quarters[j]], scaled[:, quarters[j]], ident[:])
+                nc.tensor.transpose(back[:, quarters[j]], scaled[:, q - 1, quarters[j]], ident[:])
             return back[:].rearrange("p (j i) -> p j i", j=LANES)
 
         for b in range(3):
@@ -195,24 +202,30 @@ def tile_attend_grag_d_pl_kernel(tc, xT, dT, us, ts, lk, wt, offs, out_0, out_1,
         scale_scores(4)
         row_max(2)
         row_max(3)
+        by_slot = [turn(0), turn(1)]
+        scaled = sb.tile([P, LANES - 1, BANK], F32, name="scaled", tag="neg_max3")
+        for q in range(1, LANES):
+            scale_turned(0, q)
         lik_sum(0)
         lik_sum(1)
         nc.vector.reciprocal(t1_inv[:], t1[:])
         nc.vector.reciprocal(h_scale[0][:], t2[0][:])
         nc.vector.tensor_tensor(h_bias[:], t1_inv[:], wu[:], ALU.mult)
         factors(0, halves[0])
+        products = [et[:]]
+        for q in range(1, LANES):
+            scale_turned(1, q)
+            products.append(turn_back(q))
         lik_sum(2)
         lik_sum(3)
-        products = [et[:, :, quarters[0]], et[:, :, quarters[1]], turned_product(2)]
-        factors(0, quarters[2])
         scaled_e(0)
         nc.vector.reciprocal(h_scale[1][:], t2[1][:])
         scaled_e(1)
-        factors(1, quarters[0])
-        factors(1, quarters[1])
-        products.append(turned_product(3))
+        for q in range(2):
+            for j in range(2, LANES):
+                nc.vector.tensor_scalar(hh[:, j, quarters[q]], lkw[:, j, quarters[q]], h_scale[1][:, j - 2 : j - 1], h_bias[:, j : j + 1], ALU.mult, ALU.add)
+        factors(0, halves[1])
         factors(1, quarters[2])
-        factors(0, quarters[3])
         factors(1, quarters[3])
 
         g = sb.tile([P, SLOTS * LANES], BF16, name="g", align_bytes=64)
@@ -240,8 +253,9 @@ def tile_attend_grag_d_pl_kernel(tc, xT, dT, us, ts, lk, wt, offs, out_0, out_1,
         quantise_gradient(0, half)
         early = bank(0, "early")
         table_gradient(early, 0, 0)
-        nc.scalar.copy(out=dd[0][:, halves[0]], in_=early[:, halves[1]])
         gradient(3)
+        dd_early = sb.tile([P, half], F32, name="dd_early", tag="hh")
+        nc.scalar.copy(out=dd_early[:], in_=early[:, halves[1]])
         quantise_gradient(half, half + quarter)
         quantise_gradient(half + quarter, SLOTS)
 
@@ -255,14 +269,14 @@ def tile_attend_grag_d_pl_kernel(tc, xT, dT, us, ts, lk, wt, offs, out_0, out_1,
             nc.scalar.copy(out=dst, in_=src)
 
         for j in range(LANES):
-            acc = bank(2 + j, "grad%d" % j)
+            acc = bank(3 + j, "grad%d" % j)
             table_gradient(acc, j, half)
             todo = halves[1] if j == 0 else slice(0, SLOTS)
             nc.scalar.copy(out=dd[j][:, todo], in_=acc[:, todo])
         for j in range(LANES):
             if j == 0:
                 for h in range(2):
-                    nc.vector.tensor_copy(windows[j][:].indirect(offsets[:, 16 * h : 16 * (h + 1)]), dd[j][:, halves[h]])
+                    nc.vector.tensor_copy(windows[j][:].indirect(offsets[:, 16 * h : 16 * (h + 1)]), dd[j][:, halves[h]] if h else dd_early[:])
             else:
                 nc.vector.tensor_copy(windows[j][:].indirect(offsets[:]), dd[j][:])
             nc.sync.dma_start(out=out_rows[:, j, :], in_=windows[j][:])

@@ -25,10 +25,9 @@ RUN = 4
 GRAIN = 128
 GRAINS = DOCS // GRAIN
 PER_BANK = BANK // GRAIN
-GROUPS = [(0, 1), (1, 2), (2, 4), (4, 6), (6, 8), (8, 10), (10, 12), (12, 13), (13, 15), (15, 16)]
-SCALAR_WEAVES = 2
+GROUPS = [(0, 2), (2, 4), (4, 6), (6, 8), (8, 10), (10, 12), (12, 14), (14, 15), (15, 16)]
+VECTOR_GRAINS = 4
 STORES = {4: 0, 8: 4, 12: 8, 15: 12, 16: 15}
-LATE = 14
 
 
 def tile_attend_grag_d_pl_kernel(tc, xT, dT, us, ts, lk, wt, offs, out_0, out_1, out_2):
@@ -99,10 +98,8 @@ def tile_attend_grag_d_pl_kernel(tc, xT, dT, us, ts, lk, wt, offs, out_0, out_1,
 
         half = SLOTS // 2
         halves = [slice(half * h, half * (h + 1)) for h in range(2)]
-        g_codes = sb.tile([P, half + SLOTS], U32, name="g_codes", align_bytes=64)
-        g_scales = sb.tile([P, half + SLOTS], U8, name="g_scales", align_bytes=64)
-        nc.gpsimd.memset(g_codes[:, 0:half], 0)
-        nc.gpsimd.memset(g_scales[:, 0:half], 0)
+        g_codes = sb.tile([P, SLOTS], U32, name="g_codes", align_bytes=64)
+        g_scales = sb.tile([P, SLOTS], U8, name="g_scales", align_bytes=64)
         dg_flat = sb.tile([P, 2 * SLOTS], BF16, name="dg_flat", tag="ts_all")
         for t in range(2):
             nc.vector.tensor_copy(dg_flat[:, SLOTS * t : SLOTS * (t + 1)], docs[t][:].indirect(offsets[:]))
@@ -228,7 +225,7 @@ def tile_attend_grag_d_pl_kernel(tc, xT, dT, us, ts, lk, wt, offs, out_0, out_1,
         factors(1, quarters[2])
         factors(1, quarters[3])
 
-        g = sb.tile([P, SLOTS * LANES], BF16, name="g", align_bytes=64)
+        g = sb.tile([P, SLOTS * LANES], BF16, name="g", tag="g", align_bytes=64)
 
         def gradient(q):
             nc.vector.tensor_tensor(g[:, BANK * q : BANK * (q + 1)].rearrange("p (c i j) -> p c j i", i=RUN, j=LANES),
@@ -236,59 +233,84 @@ def tile_attend_grag_d_pl_kernel(tc, xT, dT, us, ts, lk, wt, offs, out_0, out_1,
                                     hh[:, :, quarters[q]].rearrange("p j (c i) -> p c j i", i=RUN), ALU.mult)
 
         def quantise_gradient(i0, i1):
-            nc.vector.quantize_mx(out=g_codes[:, half + i0 : half + i1].bitcast(E5M2X4), scales=g_scales[:, half + i0 : half + i1],
+            nc.vector.quantize_mx(out=g_codes[:, i0:i1].bitcast(E5M2X4), scales=g_scales[:, i0:i1],
                                   in_=g[:, LANES * i0 : LANES * i1])
 
-        def table_gradient(acc, j, first):
+        def table_gradient(b, j, slots):
             cols = slice(P * j, P * (j + 1))
-            nc.tensor.matmul_mx(out=acc[:], lhsT=xr_codes[:, cols].bitcast(E4M3X4), lhsT_scale=xr_scales[:, cols],
-                                rhs=g_codes[:, first : first + SLOTS].bitcast(E5M2X4), rhs_scale=g_scales[:, first : first + SLOTS],
-                                start=True, stop=True)
+            acc = bank(b, "grad%d_%d" % (j, slots.start))
+            nc.tensor.matmul_mx(out=acc[:, slots], lhsT=xr_codes[:, cols].bitcast(E4M3X4), lhsT_scale=xr_scales[:, cols],
+                                rhs=g_codes[:, slots].bitcast(E5M2X4), rhs_scale=g_scales[:, slots], start=True, stop=True)
+            return acc
 
-        dd = [sb.tile([P, SLOTS], F32, name="dd%d" % j) for j in range(LANES)]
         quarter = SLOTS // 4
         gradient(0)
         gradient(1)
         gradient(2)
         quantise_gradient(0, half)
-        early = bank(0, "early")
-        table_gradient(early, 0, 0)
+        early = [table_gradient(b, j, halves[0]) for j, b in ((0, 0), (1, 3))]
         gradient(3)
-        dd_early = sb.tile([P, half], F32, name="dd_early", tag="hh")
-        nc.scalar.copy(out=dd_early[:], in_=early[:, halves[1]])
         quantise_gradient(half, half + quarter)
         quantise_gradient(half + quarter, SLOTS)
+        late = [table_gradient(b, j, halves[1]) for j, b in ((0, 4), (1, 5))]
+        whole = [table_gradient(b, j, slice(0, SLOTS)) for j, b in ((2, 6), (3, 7))]
 
         out_rows = out_0.rearrange("(p j) c -> p j c", j=LANES)
-        pairs = sb.tile([P, DOCS * LANES], BF16, name="pairs")
+        lists = [offsets[:, 16 * h : 16 * (h + 1)] for h in range(2)]
+
+        def scatter_scalar(j, h, src):
+            nc.scalar.activation(windows[j][:].indirect(lists[h]), src, ACT.Copy)
+
+        def scatter_vector(j, h, src):
+            nc.vector.tensor_copy(windows[j][:].indirect(lists[h]), src)
+
+        def store(j):
+            (nc.sync if j == 1 else nc.scalar).dma_start(out=out_rows[:, j, :], in_=windows[j][:])
+
+        dd0 = sb.tile([P, SLOTS], F32, name="dd0", tag="dd0")
+        dd1 = sb.tile([P, SLOTS], F32, name="dd1", tag="g", align_bytes=64)
+        dd3 = sb.tile([P, half], F32, name="dd3", tag="dd3_0")
+        nc.scalar.copy(out=dd0[:, halves[0]], in_=early[0][:, halves[0]])
+        scatter_scalar(0, 0, dd0[:, halves[0]])
+        nc.vector.tensor_copy(out=dd1[:, halves[0]], in_=early[1][:, halves[0]])
+        scatter_vector(1, 0, dd1[:, halves[0]])
+        nc.scalar.copy(out=dd0[:, halves[1]], in_=late[0][:, halves[1]])
+        scatter_scalar(0, 1, dd0[:, halves[1]])
+        store(0)
+        nc.vector.tensor_copy(out=dd1[:, halves[1]], in_=late[1][:, halves[1]])
+        nc.vector.tensor_copy(out=dd3[:], in_=whole[1][:, halves[0]])
+        scatter_vector(1, 1, dd1[:, halves[1]])
+        store(1)
+        dd2 = sb.tile([P, SLOTS], F32, name="dd2", tag="dd0")
+        nc.scalar.copy(out=dd2[:], in_=whole[0][:])
+        for h in range(2):
+            scatter_scalar(2, h, dd2[:, halves[h]])
+        store(2)
+        scatter_vector(3, 0, dd3[:])
+        dd3_late = sb.tile([P, half], F32, name="dd3_late", tag="dd0")
+        nc.scalar.copy(out=dd3_late[:], in_=whole[1][:, halves[1]])
+        scatter_scalar(3, 1, dd3_late[:])
+        store(3)
+
+        pairs = sb.tile([P, DOCS * LANES], BF16, name="pairs", tag="dd3_0")
         pair_lanes = pairs[:].rearrange("p (k u c e) -> p k u c e", u=2, c=GRAIN, e=2)
 
-        def round_lane(j, k0, k1):
+        def round_lane(j, k0, k1, on_scalar):
             dst = pair_lanes[:, k0:k1, j // 2, :, j % 2]
             src = windows[j][:, GRAIN * k0 : GRAIN * k1].rearrange("p (k c) -> p k c", c=GRAIN)
-            nc.scalar.copy(out=dst, in_=src)
+            if on_scalar:
+                nc.scalar.copy(out=dst, in_=src)
+            else:
+                nc.vector.tensor_copy(out=dst, in_=src)
 
-        for j in range(LANES):
-            acc = bank(3 + j, "grad%d" % j)
-            table_gradient(acc, j, half)
-            todo = halves[1] if j == 0 else slice(0, SLOTS)
-            nc.scalar.copy(out=dd[j][:, todo], in_=acc[:, todo])
-        for j in range(LANES):
-            if j == 0:
-                for h in range(2):
-                    nc.vector.tensor_copy(windows[j][:].indirect(offsets[:, 16 * h : 16 * (h + 1)]), dd[j][:, halves[h]] if h else dd_early[:])
-            else:
-                nc.vector.tensor_copy(windows[j][:].indirect(offsets[:]), dd[j][:])
-            nc.sync.dma_start(out=out_rows[:, j, :], in_=windows[j][:])
-            if j < LANES - 2:
-                round_lane(j, 0, GRAINS)
-            elif j == LANES - 2:
-                round_lane(j, 0, LATE)
-            else:
-                for k0, k1 in GROUPS[:-SCALAR_WEAVES]:
-                    round_lane(j, k0, k1)
-                round_lane(j - 1, LATE, GRAINS)
-                round_lane(j, GROUPS[-SCALAR_WEAVES][0], GRAINS)
+        for j in range(2):
+            round_lane(j, 0, GRAINS, False)
+        for j in range(2, LANES):
+            round_lane(j, 0, VECTOR_GRAINS, False)
+        for k0, k1 in GROUPS:
+            if k0 >= VECTOR_GRAINS:
+                for j in range(2, LANES):
+                    round_lane(j, k0, k1, True)
 
         words_out = out_1.rearrange("a p c l -> p (a c l)").bitcast(I32)
         scales_out = out_2.rearrange("o f (a c) -> a (o f) c", c=BANK).bitcast(I32)
@@ -299,14 +321,9 @@ def tile_attend_grag_d_pl_kernel(tc, xT, dT, us, ts, lk, wt, offs, out_0, out_1,
         def weave(n):
             k0, k1 = GROUPS[n]
             span = slice(GRAIN * LANES * k0, GRAIN * LANES * k1)
-            on_scalar = n >= len(GROUPS) - SCALAR_WEAVES
-            word = U32 if on_scalar else I32
-            dst = woven[:, span].bitcast(word).rearrange("p (k c u) -> p k c u", c=GRAIN, u=2)
-            src = pairs[:, span].bitcast(word).rearrange("p (k u c) -> p k c u", c=GRAIN, u=2)
-            if on_scalar:
-                nc.scalar.copy(out=dst, in_=src)
-            else:
-                nc.vector.tensor_copy(out=dst, in_=src)
+            dst = woven[:, span].bitcast(I32).rearrange("p (k c u) -> p k c u", c=GRAIN, u=2)
+            src = pairs[:, span].bitcast(I32).rearrange("p (k u c) -> p k c u", c=GRAIN, u=2)
+            nc.vector.tensor_copy(out=dst, in_=src)
 
         def quantise(n):
             k0, k1 = GROUPS[n]

@@ -26,7 +26,8 @@ GRAIN = 128
 GRAINS = DOCS // GRAIN
 PER_BANK = BANK // GRAIN
 GROUPS = [(0, 2), (2, 4), (4, 6), (6, 8), (8, 10), (10, 12), (12, 14), (14, 15), (15, 16)]
-VECTOR_GRAINS = 4
+VECTOR_GRAINS = 2
+GPSIMD_GRAINS = 12
 STORES = {4: 0, 8: 4, 12: 8, 15: 12, 16: 15}
 
 
@@ -253,7 +254,7 @@ def tile_attend_grag_d_pl_kernel(tc, xT, dT, us, ts, lk, wt, offs, out_0, out_1,
         quantise_gradient(half, half + quarter)
         quantise_gradient(half + quarter, SLOTS)
         late = [table_gradient(b, j, halves[1]) for j, b in ((0, 4), (1, 5))]
-        whole = [table_gradient(b, j, slice(0, SLOTS)) for j, b in ((2, 6), (3, 7))]
+        whole = [table_gradient(b, j, slice(0, SLOTS)) for j, b in ((3, 7), (2, 6))]
 
         out_rows = out_0.rearrange("(p j) c -> p j c", j=LANES)
         lists = [offsets[:, 16 * h : 16 * (h + 1)] for h in range(2)]
@@ -265,52 +266,53 @@ def tile_attend_grag_d_pl_kernel(tc, xT, dT, us, ts, lk, wt, offs, out_0, out_1,
             nc.vector.tensor_copy(windows[j][:].indirect(lists[h]), src)
 
         def store(j):
-            (nc.sync if j == 1 else nc.scalar).dma_start(out=out_rows[:, j, :], in_=windows[j][:])
+            (nc.sync if j % 2 else nc.scalar).dma_start(out=out_rows[:, j, :], in_=windows[j][:])
 
         dd0 = sb.tile([P, SLOTS], F32, name="dd0", tag="dd0")
         dd1 = sb.tile([P, SLOTS], F32, name="dd1", tag="g", align_bytes=64)
-        dd3 = sb.tile([P, half], F32, name="dd3", tag="dd3_0")
+        dd3 = sb.tile([P, SLOTS], F32, name="dd3")
         nc.scalar.copy(out=dd0[:, halves[0]], in_=early[0][:, halves[0]])
         scatter_scalar(0, 0, dd0[:, halves[0]])
         nc.vector.tensor_copy(out=dd1[:, halves[0]], in_=early[1][:, halves[0]])
+        nc.vector.tensor_copy(out=dd0[:, halves[1]], in_=late[0][:, halves[1]])
         scatter_vector(1, 0, dd1[:, halves[0]])
-        nc.scalar.copy(out=dd0[:, halves[1]], in_=late[0][:, halves[1]])
         scatter_scalar(0, 1, dd0[:, halves[1]])
         store(0)
         nc.vector.tensor_copy(out=dd1[:, halves[1]], in_=late[1][:, halves[1]])
-        nc.vector.tensor_copy(out=dd3[:], in_=whole[1][:, halves[0]])
+        nc.vector.tensor_copy(out=dd3[:], in_=whole[0][:])
         scatter_vector(1, 1, dd1[:, halves[1]])
         store(1)
+        nc.vector.tensor_copy(windows[3][:].indirect(offsets[:]), dd3[:])
         dd2 = sb.tile([P, SLOTS], F32, name="dd2", tag="dd0")
-        nc.scalar.copy(out=dd2[:], in_=whole[0][:])
+        nc.scalar.copy(out=dd2[:], in_=whole[1][:])
         for h in range(2):
             scatter_scalar(2, h, dd2[:, halves[h]])
         store(2)
-        scatter_vector(3, 0, dd3[:])
-        dd3_late = sb.tile([P, half], F32, name="dd3_late", tag="dd0")
-        nc.scalar.copy(out=dd3_late[:], in_=whole[1][:, halves[1]])
-        scatter_scalar(3, 1, dd3_late[:])
         store(3)
 
-        pairs = sb.tile([P, DOCS * LANES], BF16, name="pairs", tag="dd3_0")
+        pairs = sb.tile([P, DOCS * LANES], BF16, name="pairs")
         pair_lanes = pairs[:].rearrange("p (k u c e) -> p k u c e", u=2, c=GRAIN, e=2)
 
-        def round_lane(j, k0, k1, on_scalar):
+        def round_lane(j, k0, k1, engine):
             dst = pair_lanes[:, k0:k1, j // 2, :, j % 2]
             src = windows[j][:, GRAIN * k0 : GRAIN * k1].rearrange("p (k c) -> p k c", c=GRAIN)
-            if on_scalar:
+            if engine == "scalar":
                 nc.scalar.copy(out=dst, in_=src)
-            else:
+            elif engine == "vector":
                 nc.vector.tensor_copy(out=dst, in_=src)
+            else:
+                nc.gpsimd.tensor_scalar(dst, src, 1.0, 1.0, ALU.mult, ALU.mult)
 
         for j in range(2):
-            round_lane(j, 0, GRAINS, False)
+            round_lane(j, 0, GPSIMD_GRAINS, "gpsimd")
+        for j in range(2):
+            round_lane(j, GPSIMD_GRAINS, GRAINS, "scalar")
         for j in range(2, LANES):
-            round_lane(j, 0, VECTOR_GRAINS, False)
+            round_lane(j, 0, VECTOR_GRAINS, "vector")
         for k0, k1 in GROUPS:
             if k0 >= VECTOR_GRAINS:
                 for j in range(2, LANES):
-                    round_lane(j, k0, k1, True)
+                    round_lane(j, k0, k1, "scalar")
 
         words_out = out_1.rearrange("a p c l -> p (a c l)").bitcast(I32)
         scales_out = out_2.rearrange("o f (a c) -> a (o f) c", c=BANK).bitcast(I32)

@@ -26,7 +26,7 @@ GRAIN = 128
 GRAINS = DOCS // GRAIN
 PER_BANK = BANK // GRAIN
 GROUPS = [(0, 2), (2, 4), (4, 6), (6, 8), (8, 10), (10, 12), (12, 14), (14, 15), (15, 16)]
-VECTOR_GRAINS = 2
+VECTOR_GRAINS = 4
 GPSIMD_GRAINS = 12
 STORES = {4: 0, 8: 4, 12: 8, 15: 12, 16: 15}
 
@@ -226,35 +226,38 @@ def tile_attend_grag_d_pl_kernel(tc, xT, dT, us, ts, lk, wt, offs, out_0, out_1,
         factors(1, quarters[2])
         factors(1, quarters[3])
 
-        g = sb.tile([P, SLOTS * LANES], BF16, name="g", tag="g", align_bytes=64)
+        g = [sb.tile([P, half * LANES], BF16, name="g%d" % h, tag="g", align_bytes=64) for h in range(2)]
 
         def gradient(q):
-            nc.vector.tensor_tensor(g[:, BANK * q : BANK * (q + 1)].rearrange("p (c i j) -> p c j i", i=RUN, j=LANES),
+            nc.vector.tensor_tensor(g[q // 2][:, BANK * (q % 2) : BANK * (q % 2 + 1)].rearrange("p (c i j) -> p c j i", i=RUN, j=LANES),
                                     products[q].rearrange("p j (c i) -> p c j i", i=RUN),
                                     hh[:, :, quarters[q]].rearrange("p j (c i) -> p c j i", i=RUN), ALU.mult)
 
         def quantise_gradient(i0, i1):
             nc.vector.quantize_mx(out=g_codes[:, i0:i1].bitcast(E5M2X4), scales=g_scales[:, i0:i1],
-                                  in_=g[:, LANES * i0 : LANES * i1])
+                                  in_=g[i0 // half][:, LANES * (i0 % half) : LANES * (i0 % half + i1 - i0)])
 
-        def table_gradient(b, j, slots):
+        def table_gradient(acc, j, slots):
             cols = slice(P * j, P * (j + 1))
-            acc = bank(b, "grad%d_%d" % (j, slots.start))
-            nc.tensor.matmul_mx(out=acc[:, slots], lhsT=xr_codes[:, cols].bitcast(E4M3X4), lhsT_scale=xr_scales[:, cols],
+            nc.tensor.matmul_mx(out=acc, lhsT=xr_codes[:, cols].bitcast(E4M3X4), lhsT_scale=xr_scales[:, cols],
                                 rhs=g_codes[:, slots].bitcast(E5M2X4), rhs_scale=g_scales[:, slots], start=True, stop=True)
-            return acc
 
+        grad = {name: bank(b, "grad_" + name) for name, b in (("a0", 0), ("a1a3", 3), ("b0", 4), ("b1b3", 5), ("two", 6))}
         quarter = SLOTS // 4
         gradient(0)
         gradient(1)
+        quantise_gradient(0, quarter)
+        quantise_gradient(quarter, half)
+        for name, place, j in (("a0", 0, 0), ("a1a3", 0, 1), ("a1a3", 1, 3)):
+            table_gradient(grad[name][:, halves[place]], j, halves[0])
         gradient(2)
-        quantise_gradient(0, half)
-        early = [table_gradient(b, j, halves[0]) for j, b in ((0, 0), (1, 3))]
         gradient(3)
         quantise_gradient(half, half + quarter)
         quantise_gradient(half + quarter, SLOTS)
-        late = [table_gradient(b, j, halves[1]) for j, b in ((0, 4), (1, 5))]
-        whole = [table_gradient(b, j, slice(0, SLOTS)) for j, b in ((3, 7), (2, 6))]
+        table_gradient(grad["b0"][:, halves[0]], 0, halves[1])
+        table_gradient(grad["b1b3"][:, halves[0]], 1, halves[1])
+        table_gradient(grad["b1b3"][:, halves[1]], 3, halves[1])
+        table_gradient(grad["two"][:], 2, slice(0, SLOTS))
 
         out_rows = out_0.rearrange("(p j) c -> p j c", j=LANES)
         lists = [offsets[:, 16 * h : 16 * (h + 1)] for h in range(2)]
@@ -262,29 +265,27 @@ def tile_attend_grag_d_pl_kernel(tc, xT, dT, us, ts, lk, wt, offs, out_0, out_1,
         def scatter_scalar(j, h, src):
             nc.scalar.activation(windows[j][:].indirect(lists[h]), src, ACT.Copy)
 
-        def scatter_vector(j, h, src):
-            nc.vector.tensor_copy(windows[j][:].indirect(lists[h]), src)
+        def scatter_vector(j, src):
+            nc.vector.tensor_copy(windows[j][:].indirect(offsets[:]), src)
 
         def store(j):
-            (nc.sync if j % 2 else nc.scalar).dma_start(out=out_rows[:, j, :], in_=windows[j][:])
+            (nc.scalar if j == 2 else nc.sync).dma_start(out=out_rows[:, j, :], in_=windows[j][:])
 
-        dd0 = sb.tile([P, SLOTS], F32, name="dd0", tag="dd0")
-        dd1 = sb.tile([P, SLOTS], F32, name="dd1", tag="g", align_bytes=64)
-        dd3 = sb.tile([P, SLOTS], F32, name="dd3")
-        nc.scalar.copy(out=dd0[:, halves[0]], in_=early[0][:, halves[0]])
-        scatter_scalar(0, 0, dd0[:, halves[0]])
-        nc.vector.tensor_copy(out=dd1[:, halves[0]], in_=early[1][:, halves[0]])
-        nc.vector.tensor_copy(out=dd0[:, halves[1]], in_=late[0][:, halves[1]])
-        scatter_vector(1, 0, dd1[:, halves[0]])
-        scatter_scalar(0, 1, dd0[:, halves[1]])
+        dd_a0 = sb.tile([P, half], F32, name="dd_a0")
+        dd_b0 = sb.tile([P, half], F32, name="dd_b0", tag="dd_b0")
+        dd = sb.tile([P, 2, SLOTS], F32, name="dd", tag="g", align_bytes=64)
+        nc.scalar.copy(out=dd_a0[:], in_=grad["a0"][:, halves[0]])
+        scatter_scalar(0, 0, dd_a0[:])
+        nc.vector.tensor_copy(out=dd[:, :, halves[0]], in_=grad["a1a3"][:].rearrange("p (n i) -> p n i", n=2))
+        nc.vector.tensor_copy(out=dd_b0[:], in_=grad["b0"][:, halves[0]])
+        scatter_scalar(0, 1, dd_b0[:])
         store(0)
-        nc.vector.tensor_copy(out=dd1[:, halves[1]], in_=late[1][:, halves[1]])
-        nc.vector.tensor_copy(out=dd3[:], in_=whole[0][:])
-        scatter_vector(1, 1, dd1[:, halves[1]])
+        nc.vector.tensor_copy(out=dd[:, :, halves[1]], in_=grad["b1b3"][:].rearrange("p (n i) -> p n i", n=2))
+        scatter_vector(1, dd[:, 0, :])
         store(1)
-        nc.vector.tensor_copy(windows[3][:].indirect(offsets[:]), dd3[:])
-        dd2 = sb.tile([P, SLOTS], F32, name="dd2", tag="dd0")
-        nc.scalar.copy(out=dd2[:], in_=whole[1][:])
+        scatter_vector(3, dd[:, 1, :])
+        dd2 = sb.tile([P, SLOTS], F32, name="dd2", tag="dd_b0")
+        nc.scalar.copy(out=dd2[:], in_=grad["two"][:])
         for h in range(2):
             scatter_scalar(2, h, dd2[:, halves[h]])
         store(2)

@@ -27,7 +27,7 @@ GRAINS = DOCS // GRAIN
 PER_BANK = BANK // GRAIN
 GROUPS = [(0, 2), (2, 4), (4, 6), (6, 8), (8, 10), (10, 12), (12, 14), (14, 15), (15, 16)]
 VECTOR_GRAINS = 4
-GPSIMD_GRAINS = 12
+GPSIMD_GRAINS = 11
 STORES = {4: 0, 8: 4, 12: 8, 15: 12, 16: 15}
 
 
@@ -226,16 +226,16 @@ def tile_attend_grag_d_pl_kernel(tc, xT, dT, us, ts, lk, wt, offs, out_0, out_1,
         factors(1, quarters[2])
         factors(1, quarters[3])
 
-        g = [sb.tile([P, half * LANES], BF16, name="g%d" % h, tag="g", align_bytes=64) for h in range(2)]
+        g = [sb.tile([P, BANK], BF16, name="g%d" % q, tag="g%d" % (0, 1, 0, 3)[q], align_bytes=64) for q in range(LANES)]
 
         def gradient(q):
-            nc.vector.tensor_tensor(g[q // 2][:, BANK * (q % 2) : BANK * (q % 2 + 1)].rearrange("p (c i j) -> p c j i", i=RUN, j=LANES),
+            nc.vector.tensor_tensor(g[q][:].rearrange("p (c i j) -> p c j i", i=RUN, j=LANES),
                                     products[q].rearrange("p j (c i) -> p c j i", i=RUN),
                                     hh[:, :, quarters[q]].rearrange("p j (c i) -> p c j i", i=RUN), ALU.mult)
 
-        def quantise_gradient(i0, i1):
-            nc.vector.quantize_mx(out=g_codes[:, i0:i1].bitcast(E5M2X4), scales=g_scales[:, i0:i1],
-                                  in_=g[i0 // half][:, LANES * (i0 % half) : LANES * (i0 % half + i1 - i0)])
+        def quantise_gradient(q):
+            nc.vector.quantize_mx(out=g_codes[:, quarters[q]].bitcast(E5M2X4), scales=g_scales[:, quarters[q]], in_=g[q][:])
+            table_gradient(grad["b0" if q // 2 else "a0"][:, quarters[q % 2]], 0, quarters[q])
 
         def table_gradient(acc, j, slots):
             cols = slice(P * j, P * (j + 1))
@@ -243,18 +243,16 @@ def tile_attend_grag_d_pl_kernel(tc, xT, dT, us, ts, lk, wt, offs, out_0, out_1,
                                 rhs=g_codes[:, slots].bitcast(E5M2X4), rhs_scale=g_scales[:, slots], start=True, stop=True)
 
         grad = {name: bank(b, "grad_" + name) for name, b in (("a0", 0), ("a1a3", 3), ("b0", 4), ("b1b3", 5), ("two", 6))}
-        quarter = SLOTS // 4
         gradient(0)
         gradient(1)
-        quantise_gradient(0, quarter)
-        quantise_gradient(quarter, half)
-        for name, place, j in (("a0", 0, 0), ("a1a3", 0, 1), ("a1a3", 1, 3)):
-            table_gradient(grad[name][:, halves[place]], j, halves[0])
+        quantise_gradient(0)
+        quantise_gradient(1)
+        for place, j in enumerate((1, 3)):
+            table_gradient(grad["a1a3"][:, halves[place]], j, halves[0])
         gradient(2)
         gradient(3)
-        quantise_gradient(half, half + quarter)
-        quantise_gradient(half + quarter, SLOTS)
-        table_gradient(grad["b0"][:, halves[0]], 0, halves[1])
+        quantise_gradient(2)
+        quantise_gradient(3)
         table_gradient(grad["b1b3"][:, halves[0]], 1, halves[1])
         table_gradient(grad["b1b3"][:, halves[1]], 3, halves[1])
         table_gradient(grad["two"][:], 2, slice(0, SLOTS))
@@ -273,19 +271,21 @@ def tile_attend_grag_d_pl_kernel(tc, xT, dT, us, ts, lk, wt, offs, out_0, out_1,
 
         dd_a0 = sb.tile([P, half], F32, name="dd_a0")
         dd_b0 = sb.tile([P, half], F32, name="dd_b0", tag="dd_b0")
-        dd = sb.tile([P, 2, SLOTS], F32, name="dd", tag="g", align_bytes=64)
+        dd = sb.tile([P, 2, SLOTS], F32, name="dd", tag="g3", align_bytes=64)
         nc.scalar.copy(out=dd_a0[:], in_=grad["a0"][:, halves[0]])
         scatter_scalar(0, 0, dd_a0[:])
         nc.vector.tensor_copy(out=dd[:, :, halves[0]], in_=grad["a1a3"][:].rearrange("p (n i) -> p n i", n=2))
         nc.vector.tensor_copy(out=dd_b0[:], in_=grad["b0"][:, halves[0]])
         scatter_scalar(0, 1, dd_b0[:])
         store(0)
-        nc.vector.tensor_copy(out=dd[:, :, halves[1]], in_=grad["b1b3"][:].rearrange("p (n i) -> p n i", n=2))
+        for n in range(2):
+            nc.vector.tensor_copy(out=dd[:, n, halves[1]], in_=grad["b1b3"][:, halves[n]])
         scatter_vector(1, dd[:, 0, :])
         store(1)
         scatter_vector(3, dd[:, 1, :])
         dd2 = sb.tile([P, SLOTS], F32, name="dd2", tag="dd_b0")
-        nc.scalar.copy(out=dd2[:], in_=grad["two"][:])
+        for h in range(2):
+            nc.scalar.copy(out=dd2[:, halves[h]], in_=grad["two"][:, halves[h]])
         for h in range(2):
             scatter_scalar(2, h, dd2[:, halves[h]])
         store(2)
@@ -308,12 +308,9 @@ def tile_attend_grag_d_pl_kernel(tc, xT, dT, us, ts, lk, wt, offs, out_0, out_1,
             round_lane(j, 0, GPSIMD_GRAINS, "gpsimd")
         for j in range(2):
             round_lane(j, GPSIMD_GRAINS, GRAINS, "scalar")
-        for j in range(2, LANES):
-            round_lane(j, 0, VECTOR_GRAINS, "vector")
         for k0, k1 in GROUPS:
-            if k0 >= VECTOR_GRAINS:
-                for j in range(2, LANES):
-                    round_lane(j, k0, k1, "scalar")
+            for j in range(2, LANES):
+                round_lane(j, k0, k1, "vector" if k0 < VECTOR_GRAINS else "scalar")
 
         words_out = out_1.rearrange("a p c l -> p (a c l)").bitcast(I32)
         scales_out = out_2.rearrange("o f (a c) -> a (o f) c", c=BANK).bitcast(I32)

@@ -112,10 +112,10 @@ def tile_attend_grag_d_pl_kernel(tc, xT, dT, us, ts, lk, wt, offs, out_0, out_1,
         for h in range(2):
             nc.scalar.copy(out=dg_lanes[:, halves[h], 0:2], in_=dg_flat[:].rearrange("p (t i) -> p i t", t=2)[:, halves[h], :])
         ts_turned = bank(6, "ts_turned")
-        for q in range(1, LANES):
+        for q in range(LANES):
             nc.tensor.transpose(ts_turned[:, P * q : P * (q + 1)], ts_g[:, P * q : P * (q + 1)], ident[:])
-        ts_slot = sb.tile([P, LANES - 1], F32, name="ts_slot")
-        nc.scalar.copy(out=ts_slot[:], in_=ts_turned[:, P:BANK:P])
+        ts_slot = sb.tile([P, LANES], F32, name="ts_slot")
+        nc.scalar.copy(out=ts_slot[:], in_=ts_turned[:, 0:BANK:P])
         nc.vector.tensor_copy(dg_lanes[:, :, LANES - 2], docs[LANES - 2][:].indirect(offsets[:]))
         for h in range(2):
             nc.vector.tensor_copy(dg_lanes[:, halves[h], LANES - 1], docs[LANES - 1][:].indirect(offsets[:, 16 * h : 16 * (h + 1)]))
@@ -150,7 +150,6 @@ def tile_attend_grag_d_pl_kernel(tc, xT, dT, us, ts, lk, wt, offs, out_0, out_1,
         lkw = sb.tile([P, LANES, SLOTS], F32, name="lkw")
         for j in range(LANES):
             nc.scalar.activation(lkw[:, j, :], lk_sb[:, j, :], ACT.Copy, scale=wu[:, j : j + 1])
-        et = sb.tile([P, LANES, P], F32, name="et")
         hh = sb.tile([P, LANES, SLOTS], F32, name="hh", tag="hh")
 
         def scale_scores(b):
@@ -171,25 +170,24 @@ def tile_attend_grag_d_pl_kernel(tc, xT, dT, us, ts, lk, wt, offs, out_0, out_1,
 
         quarters = [slice(P * q, P * (q + 1)) for q in range(LANES)]
 
-        def scaled_e(h):
-            tiles = slice(2 * h, 2 * h + 2)
-            nc.vector.tensor_tensor(et[:, tiles, :], e[:, tiles, quarters[0]], ts_g[:, quarters[0]].unsqueeze(1).to_broadcast([P, 2, P]), ALU.mult)
+        def first_half(j):
+            nc.vector.tensor_scalar(hh[:, j, halves[0]], lkw[:, j, halves[0]], h_scale[0][:, j : j + 1], h_bias[:, j : j + 1], ALU.mult, ALU.add)
 
         def turn(h):
             banks = [bank(3 + 2 * h + n, "e_by_slot%d_%d" % (h, n)) for n in range(2)]
-            places = [banks[(q - 1) // 2][:, halves[(q - 1) % 2]] for q in range(1, LANES)]
+            places = [banks[q // 2][:, halves[q % 2]] for q in range(LANES)]
             for c in range(2):
-                for q in range(1, LANES):
-                    nc.tensor.transpose(places[q - 1][:, quarters[c]], e[:, 2 * h + c, quarters[q]], ident[:])
+                for q in range(LANES):
+                    nc.tensor.transpose(places[q][:, quarters[c]], e[:, 2 * h + c, quarters[q]], ident[:])
             return places
 
         def scale_turned(h, q):
-            nc.scalar.activation(scaled[:, q - 1, halves[h]], by_slot[h][q - 1], ACT.Copy, scale=ts_slot[:, q - 1 : q])
+            nc.scalar.activation(scaled[:, q, halves[h]], by_slot[h][q], ACT.Copy, scale=ts_slot[:, q : q + 1])
 
         def turn_back(q):
-            back = bank((7, 1, 2)[q - 1], "et_by_question%d" % q)
+            back = bank((0, 7, 1, 2)[q], "et_by_question%d" % q)
             for j in range(LANES):
-                nc.tensor.transpose(back[:, quarters[j]], scaled[:, q - 1, quarters[j]], ident[:])
+                nc.tensor.transpose(back[:, quarters[j]], scaled[:, q, quarters[j]], ident[:])
             return back[:].rearrange("p (j i) -> p j i", j=LANES)
 
         for b in range(3):
@@ -201,24 +199,23 @@ def tile_attend_grag_d_pl_kernel(tc, xT, dT, us, ts, lk, wt, offs, out_0, out_1,
         row_max(2)
         row_max(3)
         by_slot = [turn(0), turn(1)]
-        scaled = sb.tile([P, LANES - 1, BANK], F32, name="scaled", tag="neg_max3")
-        for q in range(1, LANES):
+        scaled = sb.tile([P, LANES, BANK], F32, name="scaled", tag="neg_max3")
+        for q in range(LANES):
             scale_turned(0, q)
         lik_sum(0)
         lik_sum(1)
         nc.vector.reciprocal(t1_inv[:], t1[:])
         nc.vector.reciprocal(h_scale[0][:], t2[0][:])
         nc.vector.tensor_tensor(h_bias[:], t1_inv[:], wu[:], ALU.mult)
-        factors(0, halves[0])
-        products = [et[:]]
-        for q in range(1, LANES):
+        products = []
+        for q in range(LANES):
             scale_turned(1, q)
             products.append(turn_back(q))
         lik_sum(2)
         lik_sum(3)
-        scaled_e(0)
+        first_half(0)
         nc.vector.reciprocal(h_scale[1][:], t2[1][:])
-        scaled_e(1)
+        first_half(1)
         for q in range(2):
             for j in range(2, LANES):
                 nc.vector.tensor_scalar(hh[:, j, quarters[q]], lkw[:, j, quarters[q]], h_scale[1][:, j - 2 : j - 1], h_bias[:, j : j + 1], ALU.mult, ALU.add)

from contextlib import ExitStack

import concourse.mybir as mybir
from concourse.masks import make_identity

D, R, SLOTS, DOCS = 512, 512, 512, 2048
FLOPS = 2 * 2 * D * R * SLOTS

F32 = mybir.dt.float32
BF16 = mybir.dt.bfloat16
I32 = mybir.dt.int32
U32 = mybir.dt.uint32
U16 = mybir.dt.uint16
U8 = mybir.dt.uint8
E4M3X4 = mybir.dt.float8_e4m3fn_x4
E5M2X4 = mybir.dt.float8_e5m2_x4
ALU = mybir.AluOpType
ACT = mybir.ActivationFunctionType
AX = mybir.AxisListType

P = 128
LANES = 4
BANK = 512
RUN = 4
GRAIN = 128
GRAINS = DOCS // GRAIN
PER_BANK = BANK // GRAIN
GROUPS = [(0, 2), (2, 4), (4, 6), (6, 8), (8, 10), (10, 12), (12, 14), (14, 15), (15, 16)]
VECTOR_GRAINS = 4
GPSIMD_GRAINS = 11
STORES = {4: 0, 8: 4, 12: 8, 15: 12, 16: 15}


def tile_attend_grag_d_pl_kernel(tc, xT, dT, us, ts, lk, wt, offs, out_0, out_1, out_2):
    nc = tc.nc
    with ExitStack() as ctx:
        sb = ctx.enter_context(tc.tile_pool(name="sb", bufs=1))
        psum = ctx.enter_context(tc.psum_pool(name="psum", bufs=1))

        def bank(b, name):
            return psum.tile([P, BANK], F32, name=name, tag="bank%d" % b)

        offsets = sb.tile([P, SLOTS // 16], U16, name="offsets")
        x_raw = sb.tile([P, LANES, R], F32, name="x_raw")
        ts_cols = sb.tile([P, DOCS // P], F32, name="ts_cols")
        us_sb = sb.tile([P, LANES], F32, name="us_sb")
        wt_sb = sb.tile([P, LANES], F32, name="wt_sb")
        lk_sb = sb.tile([P, LANES, SLOTS], F32, name="lk_sb")
        docs = [sb.tile([P, DOCS], F32, name="docs%d" % t, tag="docs%d" % t, align_bytes=64) for t in range(LANES)]

        nc.scalar.dma_start(out=ts_cols[:], in_=ts[0:1, :].rearrange("o (p m) -> (o p) m", p=P))
        nc.sync.dma_start(out=x_raw[:], in_=xT.rearrange("(p t) r -> p t r", t=LANES))
        nc.sync.dma_start(offsets[:], offs)
        d_rows = dT.rearrange("(p t) c -> p t c", t=LANES)
        for t in range(LANES):
            nc.sync.dma_start(out=docs[t][:], in_=d_rows[:, t, :])
        nc.sync.dma_start(out=us_sb[:], in_=us.rearrange("(p j) o -> p (j o)", j=LANES))
        nc.sync.dma_start(out=wt_sb[:], in_=wt.rearrange("(p j) o -> p (j o)", j=LANES))
        nc.sync.dma_start(out=lk_sb[:], in_=lk.rearrange("(p j) i -> p j i", j=LANES))

        ident = sb.tile([P, P], F32, name="ident")
        make_identity(nc, ident[:])

        windows = [sb.tile([P, DOCS], F32, name="window%d" % j) for j in range(2)]
        for j in range(2):
            nc.vector.memset(windows[j][:].bitcast(I32), 0)

        ts_all = sb.tile([P, DOCS], F32, name="ts_all", tag="ts_all")
        per = DOCS // P
        ts_view = ts_all[:].rearrange("q (p m) -> q p m", m=per)
        for b in range(per // RUN):
            spread = bank(b, "spread%d" % b)
            for m in range(RUN):
                col = RUN * b + m
                nc.tensor.transpose(spread[:, P * m : P * (m + 1)], ts_cols[:, col : col + 1].to_broadcast([P, P]), ident[:])
            nc.scalar.copy(out=ts_view[:, :, RUN * b : RUN * (b + 1)], in_=spread[:].rearrange("q (m p) -> q p m", m=RUN))

        xd = sb.tile([P, R * LANES], BF16, name="xd", align_bytes=64)
        nc.vector.tensor_copy(out=xd[:].rearrange("p (j s t) -> p s t j", j=LANES, t=LANES),
                              in_=x_raw[:].rearrange("p t (s j) -> p s t j", j=LANES))
        xd_codes = sb.tile([P, R], U32, name="xd_codes", align_bytes=64)
        xd_scales = sb.tile([P, R], U8, name="xd_scales", align_bytes=64)
        nc.vector.quantize_mx(out=xd_codes[:].bitcast(E4M3X4), scales=xd_scales[:], in_=xd[:])

        ts_g = sb.tile([P, SLOTS], F32, name="ts_g")
        nc.vector.tensor_copy(ts_g[:], ts_all[:].indirect(offsets[:]))

        xd_words = xd[:].bitcast(F32).rearrange("p (j s u) -> p j s u", j=LANES, u=2)
        xr = sb.tile([P, D * LANES], BF16, name="xr", align_bytes=64)
        xr_view = xr[:].rearrange("s (t p j) -> s t p j", t=LANES, j=LANES)
        for u in range(2):
            turned = bank(LANES + u, "turned%d" % u)
            for j in range(LANES):
                nc.tensor.transpose(turned[:, P * j : P * (j + 1)], xd_words[:, j, :, u], ident[:])
            nc.scalar.copy(out=xr_view[:, 2 * u : 2 * u + 2], in_=turned[:].bitcast(BF16).rearrange("s (j p e) -> s e p j", j=LANES, e=2))

        wu = sb.tile([P, LANES], F32, name="wu")
        nc.gpsimd.tensor_tensor(wu[:], wt_sb[:], us_sb[:], ALU.mult)

        half = SLOTS // 2
        halves = [slice(half * h, half * (h + 1)) for h in range(2)]
        g_codes = sb.tile([P, SLOTS], U32, name="g_codes", align_bytes=64)
        g_scales = sb.tile([P, SLOTS], U8, name="g_scales", align_bytes=64)
        dg_flat = sb.tile([P, 2 * SLOTS], BF16, name="dg_flat", tag="ts_all")
        for t in range(2):
            nc.vector.tensor_copy(dg_flat[:, SLOTS * t : SLOTS * (t + 1)], docs[t][:].indirect(offsets[:]))
        xr_codes = sb.tile([P, D], U32, name="xr_codes", tag="docs0", align_bytes=64)
        xr_scales = sb.tile([P, D], U8, name="xr_scales", align_bytes=64)
        nc.vector.quantize_mx(out=xr_codes[:].bitcast(E4M3X4), scales=xr_scales[:], in_=xr[:])
        dg = sb.tile([P, SLOTS * LANES], BF16, name="dg", tag="docs1", align_bytes=64)
        dg_lanes = dg[:].rearrange("p (i t) -> p i t", t=LANES)
        for h in range(2):
            nc.scalar.copy(out=dg_lanes[:, halves[h], 0:2], in_=dg_flat[:].rearrange("p (t i) -> p i t", t=2)[:, halves[h], :])
        ts_turned = bank(6, "ts_turned")
        for q in range(LANES):
            nc.tensor.transpose(ts_turned[:, P * q : P * (q + 1)], ts_g[:, P * q : P * (q + 1)], ident[:])
        ts_slot = sb.tile([P, LANES], F32, name="ts_slot")
        nc.scalar.copy(out=ts_slot[:], in_=ts_turned[:, 0:BANK:P])
        nc.vector.tensor_copy(dg_lanes[:, :, LANES - 2], docs[LANES - 2][:].indirect(offsets[:]))
        for h in range(2):
            nc.vector.tensor_copy(dg_lanes[:, halves[h], LANES - 1], docs[LANES - 1][:].indirect(offsets[:, 16 * h : 16 * (h + 1)]))
        dg_codes = sb.tile([P, SLOTS], U32, name="dg_codes", tag="dg_codes", align_bytes=64)
        dg_scales = sb.tile([P, SLOTS], U8, name="dg_scales", align_bytes=64)
        for h in range(2):
            nc.vector.quantize_mx(out=dg_codes[:, halves[h]].bitcast(E4M3X4), scales=dg_scales[:, halves[h]],
                                  in_=dg[:, LANES * half * h : LANES * half * (h + 1)])

        def score(acc, j, slots):
            cols = slice(P * j, P * (j + 1))
            nc.tensor.matmul_mx(out=acc, lhsT=xd_codes[:, cols].bitcast(E4M3X4), lhsT_scale=xd_scales[:, cols],
                                rhs=dg_codes[:, slots].bitcast(E4M3X4), rhs_scale=dg_scales[:, slots], start=True, stop=True)

        pieces = [(0, halves[h]) for h in range(2)] + [(j, slice(0, SLOTS)) for j in range(1, LANES)]
        scores = [bank(b, "scores%d" % b) for b in range(len(pieces))]
        for b, (j, slots) in enumerate(pieces):
            score(scores[b][:, slots], j, slots)

        for j, tag in ((2, "docs1"), (3, "dg_codes")):
            windows.append(sb.tile([P, DOCS], F32, name="window%d" % j, tag=tag, align_bytes=64))
            nc.gpsimd.memset(windows[j][:].bitcast(I32), 0)

        z = [sb.tile([P, SLOTS], F32, name="z%d" % j, tag="z%d" % j) for j in range(LANES)]
        e = sb.tile([P, LANES, SLOTS], F32, name="e")
        neg_max = [sb.tile([P, 1], F32, name="neg_max%d" % j, tag="neg_max%d" % j) for j in range(LANES)]
        t1 = sb.tile([P, LANES], F32, name="t1")
        t1_inv = sb.tile([P, LANES], F32, name="t1_inv")
        h_bias = sb.tile([P, LANES], F32, name="h_bias")
        t2 = [sb.tile([P, 2], F32, name="t2_%d" % h) for h in range(2)]
        h_scale = [sb.tile([P, 2], F32, name="h_scale%d" % h) for h in range(2)]
        lkw = sb.tile([P, LANES, SLOTS], F32, name="lkw")
        for j in range(LANES):
            nc.scalar.activation(lkw[:, j, :], lk_sb[:, j, :], ACT.Copy, scale=wu[:, j : j + 1])
        hh = sb.tile([P, LANES, SLOTS], F32, name="hh", tag="hh")

        def scale_scores(b):
            j, slots = pieces[b]
            nc.vector.scalar_tensor_tensor(z[j][:, slots], scores[b][:, slots], us_sb[:, j : j + 1], ts_g[:, slots], ALU.mult, ALU.mult)

        def row_max(j):
            nc.vector.tensor_reduce(neg_max[j][:], z[j][:], AX.X, ALU.max, negate=True)
            nc.scalar.activation(e[:, j, :], z[j][:], ACT.Exp, bias=neg_max[j][:], scale=1.0, accum_out=t1[:, j : j + 1])

        def lik_sum(j):
            nc.vector.scalar_tensor_tensor(z[j][:], e[:, j, :], -1.0, lk_sb[:, j, :], ALU.mult, ALU.mult, accum_out=t2[j // 2][:, j % 2 : j % 2 + 1])

        def factors(h, slots):
            for c in range(2):
                j = 2 * h + c
                nc.scalar.activation(hh[:, j, slots], lkw[:, j, slots], ACT.Identity, bias=h_bias[:, j : j + 1], scale=h_scale[h][:, c : c + 1])

        quarters = [slice(P * q, P * (q + 1)) for q in range(LANES)]

        def first_half(j):
            nc.vector.tensor_scalar(hh[:, j, halves[0]], lkw[:, j, halves[0]], h_scale[0][:, j : j + 1], h_bias[:, j : j + 1], ALU.mult, ALU.add)

        def turn(h):
            banks = [bank(3 + 2 * h + n, "e_by_slot%d_%d" % (h, n)) for n in range(2)]
            places = [banks[q // 2][:, halves[q % 2]] for q in range(LANES)]
            for c in range(2):
                for q in range(LANES):
                    nc.tensor.transpose(places[q][:, quarters[c]], e[:, 2 * h + c, quarters[q]], ident[:])
            return places

        def scale_turned(h, q):
            nc.scalar.activation(scaled[:, q, halves[h]], by_slot[h][q], ACT.Copy, scale=ts_slot[:, q : q + 1])

        def turn_back(q):
            back = bank((0, 7, 1, 2)[q], "et_by_question%d" % q)
            for j in range(LANES):
                nc.tensor.transpose(back[:, quarters[j]], scaled[:, q, quarters[j]], ident[:])
            return back[:].rearrange("p (j i) -> p j i", j=LANES)

        for b in range(3):
            scale_scores(b)
        row_max(0)
        scale_scores(3)
        row_max(1)
        scale_scores(4)
        row_max(2)
        row_max(3)
        by_slot = [turn(0), turn(1)]
        scaled = sb.tile([P, LANES, BANK], F32, name="scaled", tag="neg_max3")
        for q in range(LANES):
            scale_turned(0, q)
        lik_sum(0)
        lik_sum(1)
        nc.vector.reciprocal(t1_inv[:], t1[:])
        nc.vector.reciprocal(h_scale[0][:], t2[0][:])
        nc.vector.tensor_tensor(h_bias[:], t1_inv[:], wu[:], ALU.mult)
        products = []
        for q in range(LANES):
            scale_turned(1, q)
            products.append(turn_back(q))
        lik_sum(2)
        lik_sum(3)
        first_half(0)
        nc.vector.reciprocal(h_scale[1][:], t2[1][:])
        first_half(1)
        for q in range(2):
            for j in range(2, LANES):
                nc.vector.tensor_scalar(hh[:, j, quarters[q]], lkw[:, j, quarters[q]], h_scale[1][:, j - 2 : j - 1], h_bias[:, j : j + 1], ALU.mult, ALU.add)
        factors(0, halves[1])
        factors(1, quarters[2])
        factors(1, quarters[3])

        g = [sb.tile([P, BANK], BF16, name="g%d" % q, tag="g%d" % (0, 1, 0, 3)[q], align_bytes=64) for q in range(LANES)]

        def gradient(q):
            nc.vector.tensor_tensor(g[q][:].rearrange("p (c i j) -> p c j i", i=RUN, j=LANES),
                                    products[q].rearrange("p j (c i) -> p c j i", i=RUN),
                                    hh[:, :, quarters[q]].rearrange("p j (c i) -> p c j i", i=RUN), ALU.mult)

        def quantise_gradient(q):
            nc.vector.quantize_mx(out=g_codes[:, quarters[q]].bitcast(E5M2X4), scales=g_scales[:, quarters[q]], in_=g[q][:])
            table_gradient(grad["b0" if q // 2 else "a0"][:, quarters[q % 2]], 0, quarters[q])

        def table_gradient(acc, j, slots):
            cols = slice(P * j, P * (j + 1))
            nc.tensor.matmul_mx(out=acc, lhsT=xr_codes[:, cols].bitcast(E4M3X4), lhsT_scale=xr_scales[:, cols],
                                rhs=g_codes[:, slots].bitcast(E5M2X4), rhs_scale=g_scales[:, slots], start=True, stop=True)

        grad = {name: bank(b, "grad_" + name) for name, b in (("a0", 0), ("a1a3", 3), ("b0", 4), ("b1b3", 5), ("two", 6))}
        gradient(0)
        gradient(1)
        quantise_gradient(0)
        quantise_gradient(1)
        for place, j in enumerate((1, 3)):
            table_gradient(grad["a1a3"][:, halves[place]], j, halves[0])
        gradient(2)
        gradient(3)
        quantise_gradient(2)
        quantise_gradient(3)
        table_gradient(grad["b1b3"][:, halves[0]], 1, halves[1])
        table_gradient(grad["b1b3"][:, halves[1]], 3, halves[1])
        table_gradient(grad["two"][:], 2, slice(0, SLOTS))

        out_rows = out_0.rearrange("(p j) c -> p j c", j=LANES)
        lists = [offsets[:, 16 * h : 16 * (h + 1)] for h in range(2)]

        def scatter_scalar(j, h, src):
            nc.scalar.activation(windows[j][:].indirect(lists[h]), src, ACT.Copy)

        def scatter_vector(j, src):
            nc.vector.tensor_copy(windows[j][:].indirect(offsets[:]), src)

        def store(j):
            (nc.scalar if j == 2 else nc.sync).dma_start(out=out_rows[:, j, :], in_=windows[j][:])

        dd_a0 = sb.tile([P, half], F32, name="dd_a0")
        dd_b0 = sb.tile([P, half], F32, name="dd_b0", tag="dd_b0")
        dd = sb.tile([P, 2, SLOTS], F32, name="dd", tag="g3", align_bytes=64)
        nc.scalar.copy(out=dd_a0[:], in_=grad["a0"][:, halves[0]])
        scatter_scalar(0, 0, dd_a0[:])
        nc.vector.tensor_copy(out=dd[:, :, halves[0]], in_=grad["a1a3"][:].rearrange("p (n i) -> p n i", n=2))
        nc.vector.tensor_copy(out=dd_b0[:], in_=grad["b0"][:, halves[0]])
        scatter_scalar(0, 1, dd_b0[:])
        store(0)
        for n in range(2):
            nc.vector.tensor_copy(out=dd[:, n, halves[1]], in_=grad["b1b3"][:, halves[n]])
        scatter_vector(1, dd[:, 0, :])
        store(1)
        scatter_vector(3, dd[:, 1, :])
        dd2 = sb.tile([P, SLOTS], F32, name="dd2", tag="dd_b0")
        for h in range(2):
            nc.scalar.copy(out=dd2[:, halves[h]], in_=grad["two"][:, halves[h]])
        for h in range(2):
            scatter_scalar(2, h, dd2[:, halves[h]])
        store(2)
        store(3)

        pairs = sb.tile([P, DOCS * LANES], BF16, name="pairs")
        pair_lanes = pairs[:].rearrange("p (k u c e) -> p k u c e", u=2, c=GRAIN, e=2)

        def round_lane(j, k0, k1, engine):
            dst = pair_lanes[:, k0:k1, j // 2, :, j % 2]
            src = windows[j][:, GRAIN * k0 : GRAIN * k1].rearrange("p (k c) -> p k c", c=GRAIN)
            if engine == "scalar":
                nc.scalar.copy(out=dst, in_=src)
            elif engine == "vector":
                nc.vector.tensor_copy(out=dst, in_=src)
            else:
                nc.gpsimd.tensor_scalar(dst, src, 1.0, 1.0, ALU.mult, ALU.mult)

        for j in range(2):
            round_lane(j, 0, GPSIMD_GRAINS, "gpsimd")
        for j in range(2):
            round_lane(j, GPSIMD_GRAINS, GRAINS, "scalar")
        for k0, k1 in GROUPS:
            for j in range(2, LANES):
                round_lane(j, k0, k1, "vector" if k0 < VECTOR_GRAINS else "scalar")

        words_out = out_1.rearrange("a p c l -> p (a c l)").bitcast(I32)
        scales_out = out_2.rearrange("o f (a c) -> a (o f) c", c=BANK).bitcast(I32)
        y_scales = sb.tile([P, BANK], U8, name="y_scales", align_bytes=64)
        woven = sb.tile([P, DOCS * LANES], BF16, name="woven", align_bytes=64)
        y_codes = sb.tile([P, DOCS], U32, name="y_codes", align_bytes=64)

        def weave(n):
            k0, k1 = GROUPS[n]
            span = slice(GRAIN * LANES * k0, GRAIN * LANES * k1)
            dst = woven[:, span].bitcast(I32).rearrange("p (k c u) -> p k c u", c=GRAIN, u=2)
            src = pairs[:, span].bitcast(I32).rearrange("p (k u c) -> p k c u", c=GRAIN, u=2)
            nc.vector.tensor_copy(out=dst, in_=src)

        def quantise(n):
            k0, k1 = GROUPS[n]
            cols = slice(GRAIN * k0, GRAIN * k1)
            nc.vector.quantize_mx(out=y_codes[:, cols].bitcast(E4M3X4), scales=y_scales[4 * (k0 // PER_BANK) : P, GRAIN * (k0 % PER_BANK) : GRAIN * (k0 % PER_BANK + k1 - k0)],
                                  in_=woven[:, GRAIN * LANES * k0 : GRAIN * LANES * k1])
            if k1 in STORES:
                first = GRAIN * STORES[k1]
                nc.sync.dma_start(out=words_out[:, first : GRAIN * k1], in_=y_codes[:, first : GRAIN * k1].bitcast(I32))

        weave(0)
        for n in range(1, len(GROUPS)):
            weave(n)
            quantise(n - 1)
        quantise(len(GROUPS) - 1)
        for q in range(4):
            eng = nc.scalar if q % 2 else nc.sync
            eng.dma_start(out=scales_out[:, 4 * q : 4 * q + 4, :], in_=y_scales[32 * q : 32 * q + 16, :].bitcast(I32))
